import numpy as np
import ml_dtypes


def mxq(x, axis, fmt="e4m3"):
    dtype, down = {"e4m3": (ml_dtypes.float8_e4m3fn, 7), "e5m2": (ml_dtypes.float8_e5m2, 14)}[fmt]
    v = np.moveaxis(np.asarray(x, np.float32).astype(ml_dtypes.bfloat16).astype(np.float64), axis, -1)
    blocks = v.reshape(v.shape[:-1] + (-1, 32))
    amax = np.abs(blocks).max(-1, keepdims=True)
    byte = np.maximum(np.where(amax > 0, np.frexp(amax)[1] - 1 + 127, 0) - down, 1)
    scale = np.exp2(byte - 127.0)
    codes = (blocks / scale).astype(np.float32).astype(dtype).astype(np.float64)
    return np.moveaxis((codes * scale).reshape(v.shape), -1, axis)


WIDE = False


def mx_kscale(k):
    if not WIDE:
        return np.ones(k)
    levels = np.array([18, -18])
    if k % 512:
        return np.exp2(np.random.permutation(np.resize(levels, k // 32))).repeat(32)
    a = np.empty((k // 512, 16))
    for p in range(k // 512):
        a[p, :8] = np.random.permutation(np.resize(levels, 8))
        for g in range(8):
            far = levels[np.abs(levels - a[p, g]) >= 10]
            a[p, g + 8] = far[np.random.randint(len(far))]
    return np.exp2(a.ravel()).repeat(32)


def f64(x):
    return np.asarray(x).astype(np.float64)


def striped(idx):
    return np.tile(np.asarray(idx).reshape(-1, 16).T, (8, 1)).astype(np.uint16)


def unstriped(offs):
    return offs[:16].T.reshape(-1).astype(np.int64)


def setup_inputs():
    n = np.random.standard_normal
    uni = np.random.uniform
    idx = np.random.permutation(2048)[:512]
    f_d = mx_kscale(512)
    f_i = np.ones(2048)
    f_i[idx] = mx_kscale(512)
    return {
        "qT": (0.5 * n((512, 512)) * f_d[:, None]).astype(np.float32),
        "kT": (n((512, 2048)) / np.sqrt(512) / f_d[:, None] * f_i[None, :]).astype(np.float32),
        "dp": (n((512, 512))).astype(np.float32),
        "us": np.tile(uni(0.75, 1.3, 512), (128, 1)).astype(np.float32),
        "ts": np.tile(uni(0.75, 1.3, 2048) / f_i, (128, 1)).astype(np.float32),
        "wt": np.tile(uni(0.75, 1.3, 512), (128, 1)).astype(np.float32),
        "offs": striped(idx),
    }


def reference(qT, kT, dp, us, ts, wt, offs):
    idx = unstriped(offs)
    kT_i = f64(kT)[:, idx]
    ts_i = f64(ts)[:1][:, idx]
    tc = ts_i.T
    a = mxq(kT_i, 0, "e4m3").T @ mxq(f64(qT), 0, "e4m3")
    z = tc * f64(us)[:1] * a
    m = (z).max(-1, keepdims=True)
    e = np.exp(z - m)
    tot = (e).sum(-1, keepdims=True)
    p = e / tot
    h = f64(wt)[:1] * f64(dp)
    c = (p * h).sum(-1, keepdims=True)
    g = tc * f64(us)[:1] * p * (h - c)
    out = mxq(kT_i, 1, "e4m3") @ mxq(g, 0, "e5m2")
    return out

@@ -1,0 +1,204 @@
+from contextlib import ExitStack
+
+import concourse.mybir as mybir
+from concourse.masks import make_identity
+
+F32 = mybir.dt.float32
+BF16 = mybir.dt.bfloat16
+U32 = mybir.dt.uint32
+U16 = mybir.dt.uint16
+U8 = mybir.dt.uint8
+E4M3 = mybir.dt.float8_e4m3fn_x4
+E5M2 = mybir.dt.float8_e5m2_x4
+ALU = mybir.AluOpType
+ACT = mybir.ActivationFunctionType
+AX = mybir.AxisListType
+
+P = 128
+PACK = 4
+D, R, SLOTS, TOKENS = 512, 512, 512, 2048
+FLOPS = 2 * 2 * D * R * SLOTS
+
+
+def tile_attend_gslot_q_kernel(tc, qT, kT, dp, us, ts, wt, offs, out):
+    nc = tc.nc
+    with ExitStack() as ctx:
+        sb = ctx.enter_context(tc.tile_pool(name="sb", bufs=1))
+        ps = ctx.enter_context(tc.psum_pool(name="ps", bufs=1))
+
+        def tiles(name, n, shape, dtype):
+            return [sb.tile(shape, dtype, name="%s%d" % (name, x), align_bytes=64) for x in range(n)]
+
+        offsets = sb.tile([P, SLOTS // 16], U16, name="offsets")
+        nc.sync.dma_start(offsets[:], offs)
+
+        q_raw = sb.tile([P, PACK, R], F32, name="q_raw")
+        nc.sync.dma_start(q_raw[:], qT.rearrange("(p j) r -> p j r", j=PACK))
+        ts_row = sb.tile([P, TOKENS], F32, name="ts_row")
+        nc.vector.memset(ts_row[:], 0.0)
+        nc.sync.dma_start(ts_row[0:1, :], ts[0:1, :])
+        k_plane = tiles("k_plane", PACK, [P, TOKENS], F32)
+        k_rows = kT.rearrange("(p j) n -> p j n", j=PACK)
+        for j in range(PACK):
+            nc.sync.dma_start(k_plane[j][:], k_rows[:, j, :])
+
+        us_sb = sb.tile([P, R], F32, name="us_sb")
+        wt_sb = sb.tile([P, R], F32, name="wt_sb")
+        dp_sb = tiles("dp_sb", PACK, [P, R], F32)
+        dp_rows = dp.rearrange("(s t) r -> s t r", t=PACK)
+        nc.sync.dma_start(us_sb[:], us)
+        nc.sync.dma_start(wt_sb[:], wt)
+        for t in range(PACK):
+            nc.sync.dma_start(dp_sb[t][:], dp_rows[:, t, :])
+
+        ident = sb.tile([P, P], F32, name="ident")
+        make_identity(nc, ident[:])
+        warm = sb.tile([P, 1], F32, name="warm")
+        nc.scalar.activation(warm[:], ident[:, 0:1], ACT.Exp)
+
+        ts_listed = sb.tile([P, SLOTS], F32, name="ts_listed")
+        nc.vector.tensor_copy(ts_listed[:], ts_row[:].indirect(offsets[:]))
+        ts_ps = ps.tile([P, PACK, P], F32, name="ts_ps")
+        for t in range(PACK):
+            nc.tensor.transpose(ts_ps[:, t, :], ts_listed[:, t::PACK], ident[:])
+        ts_col = sb.tile([P, PACK], F32, name="ts_col")
+        nc.scalar.copy(ts_col[:], ts_ps[:, :, 0])
+
+        q_words = sb.tile([P, R, PACK], BF16, name="q_words", align_bytes=64)
+        nc.vector.tensor_copy(
+            q_words[:].rearrange("p (c i) j -> p c j i", i=4),
+            q_raw[:].rearrange("p j (c i) -> p c j i", i=4),
+        )
+        q_codes = sb.tile([P, R], U32, name="q_codes", align_bytes=64)
+        q_scales = sb.tile([P, R], U8, name="q_scales", align_bytes=64)
+        nc.vector.quantize_mx(q_codes[:].bitcast(E4M3), q_scales[:], q_words[:].rearrange("p r j -> p (r j)"))
+
+        k_words = sb.tile([P, PACK, P, PACK], BF16, name="k_words", align_bytes=64)
+        for j in range(PACK):
+            nc.vector.tensor_copy(
+                k_words[:, :, :, j].rearrange("p t s -> p s t"), k_plane[j][:].indirect(offsets[:])
+            )
+        k_codes = tiles("k_codes", PACK, [P, P], U32)
+        k_scales = tiles("k_scales", PACK, [P, P], U8)
+        bank = [ps.tile([P, R], F32, name="bank%d" % t, tag="bank%d" % t) for t in range(PACK)]
+        for t in range(PACK):
+            nc.vector.quantize_mx(
+                k_codes[t][:].bitcast(E4M3), k_scales[t][:], k_words[:, t, :, :].rearrange("p s j -> p (s j)")
+            )
+            nc.tensor.matmul_mx(
+                bank[t][:], lhsT=k_codes[t][:].bitcast(E4M3), lhsT_scale=k_scales[t][:],
+                rhs=q_codes[:].bitcast(E4M3), rhs_scale=q_scales[:], start=True, stop=True,
+            )
+
+        k_pairs = k_words[:].rearrange("p t s j -> p (t s j)").bitcast(F32).rearrange("p (t s u) -> p t s u", t=PACK, u=2)
+        kt_words = sb.tile([P, D, PACK], BF16, name="kt_words", align_bytes=64)
+        kt_ps = [ps.tile([P, PACK * P], F32, name="kt_ps%d" % u) for u in range(2)]
+        for u in range(2):
+            for t in range(PACK):
+                nc.tensor.transpose(kt_ps[u][:, t * P:(t + 1) * P], k_pairs[:, t, :, u], ident[:])
+
+        def kt_evacuate(u):
+            nc.scalar.copy(
+                kt_words[:].rearrange("s (p u e) t -> s u p t e", u=2, e=2)[:, u],
+                kt_ps[u][:].bitcast(BF16).rearrange("s (t p e) -> s p t e", t=PACK, e=2),
+            )
+
+        z = tiles("z", PACK, [P, R], F32)
+        e = tiles("e", PACK, [P, R], F32)
+        h = tiles("h", PACK, [P, R], F32)
+        ph = tiles("ph", PACK, [P, R], F32)
+        neg_max = tiles("neg_max", PACK, [P, 1], F32)
+        tot = tiles("tot", PACK, [P, 1], F32)
+        rtot = tiles("rtot", PACK, [P, 1], F32)
+        tsc = tiles("tsc", PACK, [P, 1], F32)
+        coef = tiles("coef", PACK, [P, 1], F32)
+        w = sb.tile([P, PACK, R], F32, name="w")
+
+        def logits(t):
+            nc.vector.scalar_tensor_tensor(z[t][:], bank[t][:], ts_col[:, t:t + 1], us_sb[:], ALU.mult, ALU.mult)
+
+        def row_max(t):
+            nc.vector.tensor_reduce(neg_max[t][:], z[t][:], AX.X, ALU.max, negate=True)
+            nc.scalar.activation(e[t][:], z[t][:], ACT.Exp, bias=neg_max[t][:], accum_out=tot[t][:])
+
+        def gated(t):
+            nc.vector.scalar_tensor_tensor(h[t][:], dp_sb[t][:], ts_col[:, t:t + 1], wt_sb[:], ALU.mult, ALU.mult)
+
+        def recip(t):
+            nc.vector.reciprocal(rtot[t][:], tot[t][:])
+
+        def weighted(t):
+            nc.vector.scalar_tensor_tensor(ph[t][:], e[t][:], rtot[t][:], h[t][:], ALU.mult, ALU.mult, accum_out=tsc[t][:])
+
+        def coefficient(t):
+            nc.vector.tensor_scalar(coef[t][:], tsc[t][:], rtot[t][:], -1.0, ALU.mult, ALU.mult)
+
+        def centred(t):
+            nc.vector.scalar_tensor_tensor(w[:, t, :], e[t][:], coef[t][:], ph[t][:], ALU.mult, ALU.add)
+
+        kt_codes = sb.tile([P, D], U32, name="kt_codes", align_bytes=64)
+        kt_scales = sb.tile([P, D], U8, name="kt_scales", align_bytes=64)
+
+        logits(0)
+        logits(1)
+        row_max(0)
+        logits(2)
+        row_max(1)
+        kt_evacuate(0)
+        logits(3)
+        row_max(2)
+        gated(0)
+        row_max(3)
+        kt_evacuate(1)
+        recip(0)
+        gated(1)
+        weighted(0)
+        recip(1)
+        gated(2)
+        weighted(1)
+        coefficient(0)
+        recip(2)
+        gated(3)
+        centred(0)
+        weighted(2)
+        coefficient(1)
+        recip(3)
+        centred(1)
+        weighted(3)
+        coefficient(2)
+        nc.vector.quantize_mx(kt_codes[:].bitcast(E4M3), kt_scales[:], kt_words[:].rearrange("s d t -> s (d t)"))
+        coefficient(3)
+        centred(2)
+        centred(3)
+
+        g_words = sb.tile([P, R, PACK], BF16, name="g_words", align_bytes=64)
+        g_codes = sb.tile([P, R], U32, name="g_codes", align_bytes=64)
+        g_scales = sb.tile([P, R], U8, name="g_scales", align_bytes=64)
+        half = R // 2
+        for c in range(2):
+            cols = slice(c * half, (c + 1) * half)
+            nc.vector.tensor_tensor(
+                g_words[:, cols, :].rearrange("s (c i) t -> s c t i", i=2),
+                w[:, :, cols].rearrange("s t (c i) -> s c t i", i=2),
+                us_sb[:, cols].rearrange("s (c i) -> s c i", i=2).unsqueeze(2).to_broadcast([P, half // 2, PACK, 2]),
+                ALU.mult,
+            )
+        for c in range(2):
+            cols = slice(c * half, (c + 1) * half)
+            nc.vector.quantize_mx(
+                g_codes[:, cols].bitcast(E5M2), g_scales[:, cols], g_words[:, cols, :].rearrange("s r t -> s (r t)")
+            )
+
+        result = tiles("result", PACK, [P, R], F32)
+        for m in range(PACK):
+            acc = ps.tile([P, R], F32, name="acc%d" % m, tag="bank%d" % m)
+            cols = slice(m * P, (m + 1) * P)
+            nc.tensor.matmul_mx(
+                acc[:], lhsT=kt_codes[:, cols].bitcast(E4M3), lhsT_scale=kt_scales[:, cols],
+                rhs=g_codes[:].bitcast(E5M2), rhs_scale=g_scales[:], start=True, stop=True,
+            )
+            if m % 2 == 0:
+                nc.scalar.copy(result[m][:], acc[:])
+            else:
+                nc.vector.tensor_copy(result[m][:], acc[:])
+            nc.sync.dma_start(out[cols, :], result[m][:])

@@ -32,15 +32,19 @@ def tile_attend_gslot_q_kernel(tc, qT, kT, dp, us, ts, wt, offs, out):
         offsets = sb.tile([P, SLOTS // 16], U16, name="offsets")
         nc.sync.dma_start(offsets[:], offs)
 
-        q_raw = sb.tile([P, PACK, R], F32, name="q_raw")
-        nc.sync.dma_start(q_raw[:], qT.rearrange("(p j) r -> p j r", j=PACK))
         ts_row = sb.tile([P, TOKENS], F32, name="ts_row")
         nc.vector.memset(ts_row[:], 0.0)
-        nc.sync.dma_start(ts_row[0:1, :], ts[0:1, :])
         k_plane = tiles("k_plane", PACK, [P, TOKENS], F32)
         k_rows = kT.rearrange("(p j) n -> p j n", j=PACK)
         for j in range(PACK):
             nc.sync.dma_start(k_plane[j][:], k_rows[:, j, :])
+            if j == 0:
+                nc.sync.dma_start(ts_row[0:1, :], ts[0:1, :])
+        half = R // 2
+        q_raw = tiles("q_raw", 2, [P, PACK, half], F32)
+        q_rows = qT.rearrange("(p j) r -> p j r", j=PACK)
+        for c in range(2):
+            nc.sync.dma_start(q_raw[c][:], q_rows[:, :, c * half:(c + 1) * half])
 
         us_sb = sb.tile([P, R], F32, name="us_sb")
         wt_sb = sb.tile([P, R], F32, name="wt_sb")
@@ -63,55 +67,70 @@ def tile_attend_gslot_q_kernel(tc, qT, kT, dp, us, ts, wt, offs, out):
             nc.tensor.transpose(ts_ps[:, t, :], ts_listed[:, t::PACK], ident[:])
         ts_col = sb.tile([P, PACK], F32, name="ts_col")
         nc.scalar.copy(ts_col[:], ts_ps[:, :, 0])
-
-        q_words = sb.tile([P, R, PACK], BF16, name="q_words", align_bytes=64)
-        nc.vector.tensor_copy(
-            q_words[:].rearrange("p (c i) j -> p c j i", i=4),
-            q_raw[:].rearrange("p j (c i) -> p c j i", i=4),
-        )
-        q_codes = sb.tile([P, R], U32, name="q_codes", align_bytes=64)
-        q_scales = sb.tile([P, R], U8, name="q_scales", align_bytes=64)
-        nc.vector.quantize_mx(q_codes[:].bitcast(E4M3), q_scales[:], q_words[:].rearrange("p r j -> p (r j)"))
+        neg_ts_col = sb.tile([P, PACK], F32, name="neg_ts_col")
+        nc.scalar.activation(neg_ts_col[:], ts_ps[:, :, 0], ACT.Copy, scale=-1.0)
 
         k_words = sb.tile([P, PACK, P, PACK], BF16, name="k_words", align_bytes=64)
         for j in range(PACK):
             nc.vector.tensor_copy(
                 k_words[:, :, :, j].rearrange("p t s -> p s t"), k_plane[j][:].indirect(offsets[:])
             )
-        k_codes = tiles("k_codes", PACK, [P, P], U32)
-        k_scales = tiles("k_scales", PACK, [P, P], U8)
+        k_codes = sb.tile([P, SLOTS], U32, name="k_codes", align_bytes=64)
+        k_scales = sb.tile([P, SLOTS], U8, name="k_scales", align_bytes=64)
         bank = [ps.tile([P, R], F32, name="bank%d" % t, tag="bank%d" % t) for t in range(PACK)]
-        for t in range(PACK):
-            nc.vector.quantize_mx(
-                k_codes[t][:].bitcast(E4M3), k_scales[t][:], k_words[:, t, :, :].rearrange("p s j -> p (s j)")
-            )
-            nc.tensor.matmul_mx(
-                bank[t][:], lhsT=k_codes[t][:].bitcast(E4M3), lhsT_scale=k_scales[t][:],
-                rhs=q_codes[:].bitcast(E4M3), rhs_scale=q_scales[:], start=True, stop=True,
-            )
-
+        nc.vector.quantize_mx(k_codes[:].bitcast(E4M3), k_scales[:], k_words[:].rearrange("p t s j -> p (t s j)"))
         k_pairs = k_words[:].rearrange("p t s j -> p (t s j)").bitcast(F32).rearrange("p (t s u) -> p t s u", t=PACK, u=2)
-        kt_words = sb.tile([P, D, PACK], BF16, name="kt_words", align_bytes=64)
+        kt_words = tiles("kt_words", 2, [P, 2, P, PACK], BF16)
+        kt_codes = tiles("kt_codes", 2, [P, 2 * P], U32)
+        kt_scales = tiles("kt_scales", 2, [P, 2 * P], U8)
         kt_ps = [ps.tile([P, PACK * P], F32, name="kt_ps%d" % u) for u in range(2)]
-        for u in range(2):
+
+        def kt_turn(u):
             for t in range(PACK):
                 nc.tensor.transpose(kt_ps[u][:, t * P:(t + 1) * P], k_pairs[:, t, :, u], ident[:])
 
         def kt_evacuate(u):
             nc.scalar.copy(
-                kt_words[:].rearrange("s (p u e) t -> s u p t e", u=2, e=2)[:, u],
-                kt_ps[u][:].bitcast(BF16).rearrange("s (t p e) -> s p t e", t=PACK, e=2),
+                kt_words[u][:], kt_ps[u][:].bitcast(BF16).rearrange("s (t p e) -> s e p t", t=PACK, e=2)
             )
+
+        def kt_quantise(u):
+            nc.vector.quantize_mx(kt_codes[u][:].bitcast(E4M3), kt_scales[u][:], kt_words[u][:].rearrange("s e p t -> s (e p t)"))
+
+        kt_turn(0)
+        q_words = tiles("q_words", 2, [P, half, PACK], BF16)
+        q_codes = tiles("q_codes", 2, [P, half], U32)
+        q_scales = tiles("q_scales", 2, [P, half], U8)
+        for c, copy in enumerate((nc.scalar.copy, nc.vector.tensor_copy)):
+            copy(
+                q_words[c][:].rearrange("p (c i) j -> p c j i", i=4),
+                q_raw[c][:].rearrange("p j (c i) -> p c j i", i=4),
+            )
+        for c in range(2):
+            nc.vector.quantize_mx(q_codes[c][:].bitcast(E4M3), q_scales[c][:], q_words[c][:].rearrange("p r j -> p (r j)"))
+            for t in range(PACK):
+                slots = slice(t * P, (t + 1) * P)
+                nc.tensor.matmul_mx(
+                    bank[t][:, c * half:(c + 1) * half],
+                    lhsT=k_codes[:, slots].bitcast(E4M3), lhsT_scale=k_scales[:, slots],
+                    rhs=q_codes[c][:].bitcast(E4M3), rhs_scale=q_scales[c][:], start=True, stop=True,
+                )
+
+        kt_turn(1)
 
         z = tiles("z", PACK, [P, R], F32)
         e = tiles("e", PACK, [P, R], F32)
         h = tiles("h", PACK, [P, R], F32)
         ph = tiles("ph", PACK, [P, R], F32)
         neg_max = tiles("neg_max", PACK, [P, 1], F32)
-        tot = tiles("tot", PACK, [P, 1], F32)
-        rtot = tiles("rtot", PACK, [P, 1], F32)
-        tsc = tiles("tsc", PACK, [P, 1], F32)
-        coef = tiles("coef", PACK, [P, 1], F32)
+        tot = tiles("tot", 2, [P, 2], F32)
+        rtot = tiles("rtot", 2, [P, 2], F32)
+        mean = tiles("mean", 2, [P, 2], F32)
+        coef = tiles("coef", 2, [P, 2], F32)
+
+        def column(pairs, t):
+            return pairs[t // 2][:, t % 2:t % 2 + 1]
+
         w = sb.tile([P, PACK, R], F32, name="w")
 
         def logits(t):
@@ -119,68 +138,69 @@ def tile_attend_gslot_q_kernel(tc, qT, kT, dp, us, ts, wt, offs, out):
 
         def row_max(t):
             nc.vector.tensor_reduce(neg_max[t][:], z[t][:], AX.X, ALU.max, negate=True)
-            nc.scalar.activation(e[t][:], z[t][:], ACT.Exp, bias=neg_max[t][:], accum_out=tot[t][:])
+            nc.scalar.activation(e[t][:], z[t][:], ACT.Exp, bias=neg_max[t][:], accum_out=column(tot, t))
 
         def gated(t):
-            nc.vector.scalar_tensor_tensor(h[t][:], dp_sb[t][:], ts_col[:, t:t + 1], wt_sb[:], ALU.mult, ALU.mult)
+            nc.gpsimd.tensor_tensor(h[t][:], dp_sb[t][:], wt_sb[:], ALU.mult)
 
-        def recip(t):
-            nc.vector.reciprocal(rtot[t][:], tot[t][:])
+        def recip(pair):
+            nc.vector.reciprocal(rtot[pair][:], tot[pair][:])
 
         def weighted(t):
-            nc.vector.scalar_tensor_tensor(ph[t][:], e[t][:], rtot[t][:], h[t][:], ALU.mult, ALU.mult, accum_out=tsc[t][:])
+            nc.vector.scalar_tensor_tensor(
+                ph[t][:], e[t][:], column(rtot, t), h[t][:], ALU.mult, ALU.mult, accum_out=column(mean, t)
+            )
 
-        def coefficient(t):
-            nc.vector.tensor_scalar(coef[t][:], tsc[t][:], rtot[t][:], -1.0, ALU.mult, ALU.mult)
+        def coefficient(pair):
+            nc.vector.tensor_tensor(coef[pair][:], mean[pair][:], rtot[pair][:], ALU.mult)
 
         def centred(t):
-            nc.vector.scalar_tensor_tensor(w[:, t, :], e[t][:], coef[t][:], ph[t][:], ALU.mult, ALU.add)
+            nc.vector.scalar_tensor_tensor(w[:, t, :], e[t][:], column(coef, t), ph[t][:], ALU.mult, ALU.subtract)
 
-        kt_codes = sb.tile([P, D], U32, name="kt_codes", align_bytes=64)
-        kt_scales = sb.tile([P, D], U8, name="kt_scales", align_bytes=64)
+        us_ts = sb.tile([P, PACK, R], F32, name="us_ts")
 
+        def scales(t):
+            nc.scalar.activation(us_ts[:, t, :], us_sb[:], ACT.Copy, scale=neg_ts_col[:, t:t + 1])
+
+
+        for t in range(PACK):
+            gated(t)
+        kt_evacuate(0)
+        kt_quantise(0)
         logits(0)
         logits(1)
         row_max(0)
         logits(2)
         row_max(1)
-        kt_evacuate(0)
         logits(3)
         row_max(2)
-        gated(0)
+        recip(0)
         row_max(3)
         kt_evacuate(1)
-        recip(0)
-        gated(1)
+        for t in range(PACK):
+            scales(t)
         weighted(0)
-        recip(1)
-        gated(2)
         weighted(1)
+        recip(1)
         coefficient(0)
-        recip(2)
-        gated(3)
-        centred(0)
         weighted(2)
-        coefficient(1)
-        recip(3)
-        centred(1)
+        centred(0)
         weighted(3)
-        coefficient(2)
-        nc.vector.quantize_mx(kt_codes[:].bitcast(E4M3), kt_scales[:], kt_words[:].rearrange("s d t -> s (d t)"))
-        coefficient(3)
+        centred(1)
+        coefficient(1)
         centred(2)
         centred(3)
+        kt_quantise(1)
 
         g_words = sb.tile([P, R, PACK], BF16, name="g_words", align_bytes=64)
         g_codes = sb.tile([P, R], U32, name="g_codes", align_bytes=64)
         g_scales = sb.tile([P, R], U8, name="g_scales", align_bytes=64)
-        half = R // 2
         for c in range(2):
             cols = slice(c * half, (c + 1) * half)
             nc.vector.tensor_tensor(
                 g_words[:, cols, :].rearrange("s (c i) t -> s c t i", i=2),
                 w[:, :, cols].rearrange("s t (c i) -> s c t i", i=2),
-                us_sb[:, cols].rearrange("s (c i) -> s c i", i=2).unsqueeze(2).to_broadcast([P, half // 2, PACK, 2]),
+                us_ts[:, :, cols].rearrange("s t (c i) -> s c t i", i=2),
                 ALU.mult,
             )
         for c in range(2):
@@ -189,16 +209,17 @@ def tile_attend_gslot_q_kernel(tc, qT, kT, dp, us, ts, wt, offs, out):
                 g_codes[:, cols].bitcast(E5M2), g_scales[:, cols], g_words[:, cols, :].rearrange("s r t -> s (r t)")
             )
 
+        out_rows = out.rearrange("(p j) r -> p j r", j=PACK)
         result = tiles("result", PACK, [P, R], F32)
         for m in range(PACK):
             acc = ps.tile([P, R], F32, name="acc%d" % m, tag="bank%d" % m)
-            cols = slice(m * P, (m + 1) * P)
+            cols = slice(m % 2 * P, (m % 2 + 1) * P)
             nc.tensor.matmul_mx(
-                acc[:], lhsT=kt_codes[:, cols].bitcast(E4M3), lhsT_scale=kt_scales[:, cols],
+                acc[:], lhsT=kt_codes[m // 2][:, cols].bitcast(E4M3), lhsT_scale=kt_scales[m // 2][:, cols],
                 rhs=g_codes[:].bitcast(E5M2), rhs_scale=g_scales[:], start=True, stop=True,
             )
             if m % 2 == 0:
                 nc.scalar.copy(result[m][:], acc[:])
             else:
                 nc.vector.tensor_copy(result[m][:], acc[:])
-            nc.sync.dma_start(out[cols, :], result[m][:])
+            nc.sync.dma_start(out_rows[:, m, :], result[m][:])

@@ -17,6 +17,7 @@ AX = mybir.AxisListType
 P = 128
 PACK = 4
 D, R, SLOTS, TOKENS = 512, 512, 512, 2048
+HALF = R // 2
 FLOPS = 2 * 2 * D * R * SLOTS
 
 
@@ -26,28 +27,36 @@ def tile_attend_gslot_q_kernel(tc, qT, kT, dp, us, ts, wt, offs, out):
         sb = ctx.enter_context(tc.tile_pool(name="sb", bufs=1))
         ps = ctx.enter_context(tc.psum_pool(name="ps", bufs=1))
 
+        def tile(name, shape, dtype, on=None):
+            return sb.tile(shape, dtype, name=name, tag=on or name, align_bytes=64)
+
         def tiles(name, n, shape, dtype):
-            return [sb.tile(shape, dtype, name="%s%d" % (name, x), align_bytes=64) for x in range(n)]
+            return [tile("%s%d" % (name, x), shape, dtype) for x in range(n)]
+
+        def bank(name, on=None):
+            return ps.tile([P, R], F32, name=name, tag=on or name)
 
         offsets = sb.tile([P, SLOTS // 16], U16, name="offsets")
-        nc.sync.dma_start(offsets[:], offs)
 
-        ts_row = sb.tile([P, TOKENS], F32, name="ts_row")
+        ts_row = tile("ts_row", [P, TOKENS], F32)
+        wt_row = tile("wt_row", [P, R], F32)
         nc.vector.memset(ts_row[:], 0.0)
+        nc.vector.memset(wt_row[:], 0.0)
         k_plane = tiles("k_plane", PACK, [P, TOKENS], F32)
         k_rows = kT.rearrange("(p j) n -> p j n", j=PACK)
-        for j in range(PACK):
+        nc.sync.dma_start(k_plane[0][:], k_rows[:, 0, :])
+        nc.sync.dma_start(offsets[:], offs)
+        nc.sync.dma_start(k_plane[1][:], k_rows[:, 1, :])
+        nc.sync.dma_start(ts_row[0:1, :], ts[0:1, :])
+        nc.sync.dma_start(wt_row[0:1, :], wt[0:1, :])
+        for j in range(2, PACK):
             nc.sync.dma_start(k_plane[j][:], k_rows[:, j, :])
-            if j == 0:
-                nc.sync.dma_start(ts_row[0:1, :], ts[0:1, :])
-        half = R // 2
-        q_raw = tiles("q_raw", 2, [P, PACK, half], F32)
+        q_raw = tiles("q_raw", 2, [P, PACK, HALF], F32)
         q_rows = qT.rearrange("(p j) r -> p j r", j=PACK)
         for c in range(2):
-            nc.sync.dma_start(q_raw[c][:], q_rows[:, :, c * half:(c + 1) * half])
-
-        us_sb = sb.tile([P, R], F32, name="us_sb")
-        wt_sb = sb.tile([P, R], F32, name="wt_sb")
+            nc.sync.dma_start(q_raw[c][:], q_rows[:, :, c * HALF:(c + 1) * HALF])
+        us_sb = tile("us_sb", [P, R], F32)
+        wt_sb = tile("wt_sb", [P, R], F32)
         dp_sb = tiles("dp_sb", PACK, [P, R], F32)
         dp_rows = dp.rearrange("(s t) r -> s t r", t=PACK)
         nc.sync.dma_start(us_sb[:], us)
@@ -55,171 +64,207 @@ def tile_attend_gslot_q_kernel(tc, qT, kT, dp, us, ts, wt, offs, out):
         for t in range(PACK):
             nc.sync.dma_start(dp_sb[t][:], dp_rows[:, t, :])
 
-        ident = sb.tile([P, P], F32, name="ident")
+        ident = tile("ident", [P, P], F32)
         make_identity(nc, ident[:])
-        warm = sb.tile([P, 1], F32, name="warm")
+        warm = tile("warm", [P, 1], F32)
         nc.scalar.activation(warm[:], ident[:, 0:1], ACT.Exp)
 
-        ts_listed = sb.tile([P, SLOTS], F32, name="ts_listed")
-        nc.vector.tensor_copy(ts_listed[:], ts_row[:].indirect(offsets[:]))
-        ts_ps = ps.tile([P, PACK, P], F32, name="ts_ps")
-        for t in range(PACK):
-            nc.tensor.transpose(ts_ps[:, t, :], ts_listed[:, t::PACK], ident[:])
-        ts_col = sb.tile([P, PACK], F32, name="ts_col")
-        nc.scalar.copy(ts_col[:], ts_ps[:, :, 0])
-        neg_ts_col = sb.tile([P, PACK], F32, name="neg_ts_col")
-        nc.scalar.activation(neg_ts_col[:], ts_ps[:, :, 0], ACT.Copy, scale=-1.0)
+        def to_columns(name, blocks, on):
+            turned = bank(name + "_ps", on)
+            for x in range(PACK):
+                nc.tensor.transpose(turned[:, x * P:(x + 1) * P], blocks[x], ident[:])
+            columns = tile(name, [P, PACK], F32)
+            nc.scalar.copy(columns[:], turned[:, ::P])
+            return columns
 
-        k_words = sb.tile([P, PACK, P, PACK], BF16, name="k_words", align_bytes=64)
+        ts_listed = tile("ts_listed", [P, SLOTS], F32)
+        nc.vector.tensor_copy(ts_listed[:], ts_row[:].indirect(offsets[:]))
+        ts_col = to_columns("ts_col", [ts_listed[:, t::PACK] for t in range(PACK)], "h_ps0")
+        wt_col = to_columns("wt_col", [wt_row[:, b * P:(b + 1) * P] for b in range(PACK)], "h_ps1")
+
+        k_words = tile("k_words", [P, PACK, P, PACK], BF16)
         for j in range(PACK):
             nc.vector.tensor_copy(
                 k_words[:, :, :, j].rearrange("p t s -> p s t"), k_plane[j][:].indirect(offsets[:])
             )
-        k_codes = sb.tile([P, SLOTS], U32, name="k_codes", align_bytes=64)
-        k_scales = sb.tile([P, SLOTS], U8, name="k_scales", align_bytes=64)
-        bank = [ps.tile([P, R], F32, name="bank%d" % t, tag="bank%d" % t) for t in range(PACK)]
+        k_codes = tile("k_codes", [P, SLOTS], U32)
+        k_scales = tile("k_scales", [P, SLOTS], U8)
         nc.vector.quantize_mx(k_codes[:].bitcast(E4M3), k_scales[:], k_words[:].rearrange("p t s j -> p (t s j)"))
-        k_pairs = k_words[:].rearrange("p t s j -> p (t s j)").bitcast(F32).rearrange("p (t s u) -> p t s u", t=PACK, u=2)
-        kt_words = tiles("kt_words", 2, [P, 2, P, PACK], BF16)
-        kt_codes = tiles("kt_codes", 2, [P, 2 * P], U32)
-        kt_scales = tiles("kt_scales", 2, [P, 2 * P], U8)
-        kt_ps = [ps.tile([P, PACK * P], F32, name="kt_ps%d" % u) for u in range(2)]
 
-        def kt_turn(u):
+        k_pairs = k_words[:].rearrange("p t s j -> p (t s j)").bitcast(F32).rearrange("p (t s u) -> p t s u", t=PACK, u=2)
+        kt_ps, kt_words, kt_codes = {}, {}, {}
+        kt_scales = tiles("kt_scales", 2, [P, 2 * P], U8)
+
+        def kt_turn(u, on):
+            kt_ps[u] = bank("kt_ps%d" % u, on)
             for t in range(PACK):
                 nc.tensor.transpose(kt_ps[u][:, t * P:(t + 1) * P], k_pairs[:, t, :, u], ident[:])
 
-        def kt_evacuate(u):
-            nc.scalar.copy(
-                kt_words[u][:], kt_ps[u][:].bitcast(BF16).rearrange("s (t p e) -> s e p t", t=PACK, e=2)
+        def kt_evacuate(u, on):
+            kt_words[u] = tile("kt_words%d" % u, [P, 2, P, PACK], BF16, on)
+            nc.scalar.copy(kt_words[u][:], kt_ps[u][:].bitcast(BF16).rearrange("s (t p e) -> s e p t", t=PACK, e=2))
+
+        def kt_quantise(u, on):
+            kt_codes[u] = tile("kt_codes%d" % u, [P, 2 * P], U32, on)
+            nc.vector.quantize_mx(
+                kt_codes[u][:].bitcast(E4M3), kt_scales[u][:], kt_words[u][:].rearrange("s e p t -> s (e p t)")
             )
 
-        def kt_quantise(u):
-            nc.vector.quantize_mx(kt_codes[u][:].bitcast(E4M3), kt_scales[u][:], kt_words[u][:].rearrange("s e p t -> s (e p t)"))
-
-        kt_turn(0)
-        q_words = tiles("q_words", 2, [P, half, PACK], BF16)
-        q_codes = tiles("q_codes", 2, [P, half], U32)
-        q_scales = tiles("q_scales", 2, [P, half], U8)
+        kt_turn(0, None)
+        q_words = tiles("q_words", 2, [P, HALF, PACK], BF16)
+        q_codes = tiles("q_codes", 2, [P, HALF], U32)
+        q_scales = tiles("q_scales", 2, [P, HALF], U8)
         for c, copy in enumerate((nc.scalar.copy, nc.vector.tensor_copy)):
             copy(
                 q_words[c][:].rearrange("p (c i) j -> p c j i", i=4),
                 q_raw[c][:].rearrange("p j (c i) -> p c j i", i=4),
             )
+        scores = [bank("scores%d" % t) for t in range(PACK)]
         for c in range(2):
             nc.vector.quantize_mx(q_codes[c][:].bitcast(E4M3), q_scales[c][:], q_words[c][:].rearrange("p r j -> p (r j)"))
             for t in range(PACK):
                 slots = slice(t * P, (t + 1) * P)
                 nc.tensor.matmul_mx(
-                    bank[t][:, c * half:(c + 1) * half],
+                    scores[t][:, c * HALF:(c + 1) * HALF],
                     lhsT=k_codes[:, slots].bitcast(E4M3), lhsT_scale=k_scales[:, slots],
                     rhs=q_codes[c][:].bitcast(E4M3), rhs_scale=q_scales[c][:], start=True, stop=True,
                 )
 
-        kt_turn(1)
-
         z = tiles("z", PACK, [P, R], F32)
         e = tiles("e", PACK, [P, R], F32)
-        h = tiles("h", PACK, [P, R], F32)
         ph = tiles("ph", PACK, [P, R], F32)
         neg_max = tiles("neg_max", PACK, [P, 1], F32)
-        tot = tiles("tot", 2, [P, 2], F32)
-        rtot = tiles("rtot", 2, [P, 2], F32)
-        mean = tiles("mean", 2, [P, 2], F32)
-        coef = tiles("coef", 2, [P, 2], F32)
+        tot = tile("tot", [P, PACK], F32)
+        rtot = tile("rtot", [P, PACK], F32)
+        mean = tile("mean", [P, PACK], F32)
+        coef = tile("coef", [P, PACK], F32)
+        left = tile("left", [P, PACK, R], F32)
+        right = tile("right", [P, PACK, R], F32)
+        us_ts = tiles("us_ts", 3, [P, R], F32)
+        h = {}
 
-        def column(pairs, t):
-            return pairs[t // 2][:, t % 2:t % 2 + 1]
+        def column(stats, t):
+            return stats[:, t:t + 1]
 
-        w = sb.tile([P, PACK, R], F32, name="w")
+        def gate_on_gpsimd(t, on):
+            h[t] = tile("h%d" % t, [P, R], F32, on)
+            nc.gpsimd.tensor_tensor(h[t][:], dp_sb[t][:], wt_sb[:], ALU.mult)
+
+        h_turned = tiles("h_turned", 3, [P, R], F32)
+
+        def gate_turned(t):
+            dp_ps = bank("dp_ps%d" % t, "h_ps%d" % t)
+            for b in range(PACK):
+                nc.tensor.transpose(dp_ps[:, b * P:(b + 1) * P], dp_sb[t][:, b * P:(b + 1) * P], ident[:])
+            for b in range(PACK):
+                nc.scalar.activation(
+                    h_turned[t][:, b * P:(b + 1) * P], dp_ps[:, b * P:(b + 1) * P], ACT.Copy, scale=wt_col[:, b:b + 1]
+                )
+
+        def gate_turned_back(t):
+            h[t] = bank("h_ps%d" % t)
+            for b in range(PACK):
+                nc.tensor.transpose(h[t][:, b * P:(b + 1) * P], h_turned[t][:, b * P:(b + 1) * P], ident[:])
+
+        def scales(t):
+            target = us_ts[t][:] if t < 3 else right[:, t, :]
+            nc.scalar.activation(target, us_sb[:], ACT.Copy, scale=ts_col[:, t:t + 1])
 
         def logits(t):
-            nc.vector.scalar_tensor_tensor(z[t][:], bank[t][:], ts_col[:, t:t + 1], us_sb[:], ALU.mult, ALU.mult)
+            nc.vector.scalar_tensor_tensor(z[t][:], scores[t][:], ts_col[:, t:t + 1], us_sb[:], ALU.mult, ALU.mult)
 
-        def row_max(t):
+        def softmax_numerator(t):
             nc.vector.tensor_reduce(neg_max[t][:], z[t][:], AX.X, ALU.max, negate=True)
             nc.scalar.activation(e[t][:], z[t][:], ACT.Exp, bias=neg_max[t][:], accum_out=column(tot, t))
 
-        def gated(t):
-            nc.gpsimd.tensor_tensor(h[t][:], dp_sb[t][:], wt_sb[:], ALU.mult)
+        def scaled_numerator(t):
+            nc.gpsimd.tensor_tensor(right[:, t, :], e[t][:], us_ts[t][:], ALU.mult)
 
-        def recip(pair):
-            nc.vector.reciprocal(rtot[pair][:], tot[pair][:])
+        def recip(first, end):
+            nc.vector.reciprocal(rtot[:, first:end], tot[:, first:end])
 
         def weighted(t):
             nc.vector.scalar_tensor_tensor(
                 ph[t][:], e[t][:], column(rtot, t), h[t][:], ALU.mult, ALU.mult, accum_out=column(mean, t)
             )
 
-        def coefficient(pair):
-            nc.vector.tensor_tensor(coef[pair][:], mean[pair][:], rtot[pair][:], ALU.mult)
+        def coefficient(first, end):
+            nc.vector.scalar_tensor_tensor(
+                coef[:, first:end], mean[:, first:end], -1.0, rtot[:, first:end], ALU.mult, ALU.mult
+            )
 
-        def centred(t):
-            nc.vector.scalar_tensor_tensor(w[:, t, :], e[t][:], column(coef, t), ph[t][:], ALU.mult, ALU.subtract)
+        def centred_on_scalar(t):
+            nc.scalar.activation(left[:, t, :], h[t][:], ACT.Identity, bias=column(coef, t), scale=column(rtot, t))
 
-        us_ts = sb.tile([P, PACK, R], F32, name="us_ts")
+        def centred_on_vector(t):
+            nc.vector.scalar_tensor_tensor(left[:, t, :], e[t][:], column(coef, t), ph[t][:], ALU.mult, ALU.add)
 
-        def scales(t):
-            nc.scalar.activation(us_ts[:, t, :], us_sb[:], ACT.Copy, scale=neg_ts_col[:, t:t + 1])
-
-
-        for t in range(PACK):
-            gated(t)
-        kt_evacuate(0)
-        kt_quantise(0)
+        kt_evacuate(0, "q_raw0")
+        kt_quantise(0, None)
+        gate_on_gpsimd(3, "q_raw0")
         logits(0)
+        gate_turned(0)
         logits(1)
-        row_max(0)
+        softmax_numerator(0)
+        gate_turned_back(0)
+        gate_turned(1)
         logits(2)
-        row_max(1)
+        softmax_numerator(1)
+        gate_turned_back(1)
+        gate_turned(2)
         logits(3)
-        row_max(2)
-        recip(0)
-        row_max(3)
-        kt_evacuate(1)
+        softmax_numerator(2)
+        gate_turned_back(2)
+        softmax_numerator(3)
         for t in range(PACK):
             scales(t)
+        for t in range(3):
+            scaled_numerator(t)
+        kt_turn(1, "scores0")
+        recip(0, 2)
         weighted(0)
         weighted(1)
-        recip(1)
-        coefficient(0)
+        recip(2, 4)
+        coefficient(0, 2)
+        centred_on_scalar(0)
+        centred_on_scalar(1)
         weighted(2)
-        centred(0)
+        coefficient(2, 3)
+        centred_on_scalar(2)
         weighted(3)
-        centred(1)
-        coefficient(1)
-        centred(2)
-        centred(3)
-        kt_quantise(1)
+        coefficient(3, 4)
+        centred_on_vector(3)
+        kt_evacuate(1, "z3")
+        kt_quantise(1, None)
 
-        g_words = sb.tile([P, R, PACK], BF16, name="g_words", align_bytes=64)
-        g_codes = sb.tile([P, R], U32, name="g_codes", align_bytes=64)
-        g_scales = sb.tile([P, R], U8, name="g_scales", align_bytes=64)
+        g_words = tile("g_words", [P, R, PACK], BF16)
+        g_codes = tile("g_codes", [P, R], U32)
+        g_scales = tile("g_scales", [P, R], U8)
         for c in range(2):
-            cols = slice(c * half, (c + 1) * half)
+            cols = slice(c * HALF, (c + 1) * HALF)
             nc.vector.tensor_tensor(
                 g_words[:, cols, :].rearrange("s (c i) t -> s c t i", i=2),
-                w[:, :, cols].rearrange("s t (c i) -> s c t i", i=2),
-                us_ts[:, :, cols].rearrange("s t (c i) -> s c t i", i=2),
+                left[:, :, cols].rearrange("s t (c i) -> s c t i", i=2),
+                right[:, :, cols].rearrange("s t (c i) -> s c t i", i=2),
                 ALU.mult,
             )
         for c in range(2):
-            cols = slice(c * half, (c + 1) * half)
+            cols = slice(c * HALF, (c + 1) * HALF)
             nc.vector.quantize_mx(
                 g_codes[:, cols].bitcast(E5M2), g_scales[:, cols], g_words[:, cols, :].rearrange("s r t -> s (r t)")
             )
 
         out_rows = out.rearrange("(p j) r -> p j r", j=PACK)
         result = tiles("result", PACK, [P, R], F32)
-        for m in range(PACK):
-            acc = ps.tile([P, R], F32, name="acc%d" % m, tag="bank%d" % m)
-            cols = slice(m % 2 * P, (m % 2 + 1) * P)
+        for j in range(PACK):
+            acc = bank("acc%d" % j, "scores%d" % j)
+            cols = slice(j % 2 * P, (j % 2 + 1) * P)
             nc.tensor.matmul_mx(
-                acc[:], lhsT=kt_codes[m // 2][:, cols].bitcast(E4M3), lhsT_scale=kt_scales[m // 2][:, cols],
+                acc[:], lhsT=kt_codes[j // 2][:, cols].bitcast(E4M3), lhsT_scale=kt_scales[j // 2][:, cols],
                 rhs=g_codes[:].bitcast(E5M2), rhs_scale=g_scales[:], start=True, stop=True,
             )
-            if m % 2 == 0:
-                nc.scalar.copy(result[m][:], acc[:])
+            if j % 2 == 0:
+                nc.scalar.copy(result[j][:], acc[:])
             else:
-                nc.vector.tensor_copy(result[m][:], acc[:])
-            nc.sync.dma_start(out_rows[:, m, :], result[m][:])
+                nc.vector.tensor_copy(result[j][:], acc[:])
+            nc.sync.dma_start(out_rows[:, j, :], result[j][:])

@@ -18,6 +18,8 @@ P = 128
 PACK = 4
 D, R, SLOTS, TOKENS = 512, 512, 512, 2048
 HALF = R // 2
+LAST = PACK - 1
+WARM_PASSES = 2
 FLOPS = 2 * 2 * D * R * SLOTS
 
 
@@ -30,14 +32,19 @@ def tile_attend_gslot_q_kernel(tc, qT, kT, dp, us, ts, wt, offs, out):
         def tile(name, shape, dtype, on=None):
             return sb.tile(shape, dtype, name=name, tag=on or name, align_bytes=64)
 
-        def tiles(name, n, shape, dtype):
-            return [tile("%s%d" % (name, x), shape, dtype) for x in range(n)]
+        def tiles(name, count, shape, dtype):
+            return [tile("%s%d" % (name, x), shape, dtype) for x in range(count)]
 
         def bank(name, on=None):
             return ps.tile([P, R], F32, name=name, tag=on or name)
 
-        offsets = sb.tile([P, SLOTS // 16], U16, name="offsets")
+        def block(x):
+            return slice(x * P, (x + 1) * P)
 
+        def column(stats, x):
+            return stats[:, x:x + 1]
+
+        offsets = sb.tile([P, SLOTS // 16], U16, name="offsets")
         ts_row = tile("ts_row", [P, TOKENS], F32)
         wt_row = tile("wt_row", [P, R], F32)
         nc.vector.memset(ts_row[:], 0.0)
@@ -66,21 +73,19 @@ def tile_attend_gslot_q_kernel(tc, qT, kT, dp, us, ts, wt, offs, out):
 
         ident = tile("ident", [P, P], F32)
         make_identity(nc, ident[:])
-        warm = tile("warm", [P, 1], F32)
-        nc.scalar.activation(warm[:], ident[:, 0:1], ACT.Exp)
 
         def to_columns(name, blocks, on):
             turned = bank(name + "_ps", on)
             for x in range(PACK):
-                nc.tensor.transpose(turned[:, x * P:(x + 1) * P], blocks[x], ident[:])
+                nc.tensor.transpose(turned[:, block(x)], blocks[x], ident[:])
             columns = tile(name, [P, PACK], F32)
-            nc.scalar.copy(columns[:], turned[:, ::P])
+            nc.scalar.activation(columns[:], turned[:, ::P], ACT.Copy)
             return columns
 
         ts_listed = tile("ts_listed", [P, SLOTS], F32)
         nc.vector.tensor_copy(ts_listed[:], ts_row[:].indirect(offsets[:]))
         ts_col = to_columns("ts_col", [ts_listed[:, t::PACK] for t in range(PACK)], "h_ps0")
-        wt_col = to_columns("wt_col", [wt_row[:, b * P:(b + 1) * P] for b in range(PACK)], "h_ps1")
+        wt_col = to_columns("wt_col", [wt_row[:, block(b)] for b in range(PACK)], "h_ps1")
 
         k_words = tile("k_words", [P, PACK, P, PACK], BF16)
         for j in range(PACK):
@@ -92,150 +97,143 @@ def tile_attend_gslot_q_kernel(tc, qT, kT, dp, us, ts, wt, offs, out):
         nc.vector.quantize_mx(k_codes[:].bitcast(E4M3), k_scales[:], k_words[:].rearrange("p t s j -> p (t s j)"))
 
         k_pairs = k_words[:].rearrange("p t s j -> p (t s j)").bitcast(F32).rearrange("p (t s u) -> p t s u", t=PACK, u=2)
-        kt_ps, kt_words, kt_codes = {}, {}, {}
+        kt_ps, kt_words = {}, {}
+        kt_codes = tiles("kt_codes", 2, [P, 2 * P], U32)
         kt_scales = tiles("kt_scales", 2, [P, 2 * P], U8)
 
         def kt_turn(u, on):
             kt_ps[u] = bank("kt_ps%d" % u, on)
             for t in range(PACK):
-                nc.tensor.transpose(kt_ps[u][:, t * P:(t + 1) * P], k_pairs[:, t, :, u], ident[:])
+                nc.tensor.transpose(kt_ps[u][:, block(t)], k_pairs[:, t, :, u], ident[:])
 
-        def kt_evacuate(u, on):
+        def kt_copy_out(u, on):
             kt_words[u] = tile("kt_words%d" % u, [P, 2, P, PACK], BF16, on)
-            nc.scalar.copy(kt_words[u][:], kt_ps[u][:].bitcast(BF16).rearrange("s (t p e) -> s e p t", t=PACK, e=2))
+            nc.scalar.copy(kt_words[u][:], kt_ps[u][:].bitcast(BF16).rearrange("s (t p v) -> s v p t", t=PACK, v=2))
 
-        def kt_quantise(u, on):
-            kt_codes[u] = tile("kt_codes%d" % u, [P, 2 * P], U32, on)
+        def kt_quantise(u):
             nc.vector.quantize_mx(
-                kt_codes[u][:].bitcast(E4M3), kt_scales[u][:], kt_words[u][:].rearrange("s e p t -> s (e p t)")
+                kt_codes[u][:].bitcast(E4M3), kt_scales[u][:], kt_words[u][:].rearrange("s v p t -> s (v p t)")
             )
 
         kt_turn(0, None)
+
         q_words = tiles("q_words", 2, [P, HALF, PACK], BF16)
         q_codes = tiles("q_codes", 2, [P, HALF], U32)
         q_scales = tiles("q_scales", 2, [P, HALF], U8)
         for c, copy in enumerate((nc.scalar.copy, nc.vector.tensor_copy)):
             copy(
-                q_words[c][:].rearrange("p (c i) j -> p c j i", i=4),
-                q_raw[c][:].rearrange("p j (c i) -> p c j i", i=4),
+                q_words[c][:].rearrange("p (n x) j -> p n j x", x=4),
+                q_raw[c][:].rearrange("p j (n x) -> p n j x", x=4),
             )
         scores = [bank("scores%d" % t) for t in range(PACK)]
         for c in range(2):
             nc.vector.quantize_mx(q_codes[c][:].bitcast(E4M3), q_scales[c][:], q_words[c][:].rearrange("p r j -> p (r j)"))
             for t in range(PACK):
-                slots = slice(t * P, (t + 1) * P)
                 nc.tensor.matmul_mx(
                     scores[t][:, c * HALF:(c + 1) * HALF],
-                    lhsT=k_codes[:, slots].bitcast(E4M3), lhsT_scale=k_scales[:, slots],
+                    lhsT=k_codes[:, block(t)].bitcast(E4M3), lhsT_scale=k_scales[:, block(t)],
                     rhs=q_codes[c][:].bitcast(E4M3), rhs_scale=q_scales[c][:], start=True, stop=True,
                 )
 
         z = tiles("z", PACK, [P, R], F32)
         e = tiles("e", PACK, [P, R], F32)
-        ph = tiles("ph", PACK, [P, R], F32)
         neg_max = tiles("neg_max", PACK, [P, 1], F32)
         tot = tile("tot", [P, PACK], F32)
         rtot = tile("rtot", [P, PACK], F32)
-        mean = tile("mean", [P, PACK], F32)
-        coef = tile("coef", [P, PACK], F32)
         left = tile("left", [P, PACK, R], F32)
         right = tile("right", [P, PACK, R], F32)
-        us_ts = tiles("us_ts", 3, [P, R], F32)
         h = {}
 
-        def column(stats, t):
-            return stats[:, t:t + 1]
-
-        def gate_on_gpsimd(t, on):
-            h[t] = tile("h%d" % t, [P, R], F32, on)
-            nc.gpsimd.tensor_tensor(h[t][:], dp_sb[t][:], wt_sb[:], ALU.mult)
-
-        h_turned = tiles("h_turned", 3, [P, R], F32)
-
-        def gate_turned(t):
-            dp_ps = bank("dp_ps%d" % t, "h_ps%d" % t)
-            for b in range(PACK):
-                nc.tensor.transpose(dp_ps[:, b * P:(b + 1) * P], dp_sb[t][:, b * P:(b + 1) * P], ident[:])
-            for b in range(PACK):
-                nc.scalar.activation(
-                    h_turned[t][:, b * P:(b + 1) * P], dp_ps[:, b * P:(b + 1) * P], ACT.Copy, scale=wt_col[:, b:b + 1]
-                )
-
-        def gate_turned_back(t):
-            h[t] = bank("h_ps%d" % t)
-            for b in range(PACK):
-                nc.tensor.transpose(h[t][:, b * P:(b + 1) * P], h_turned[t][:, b * P:(b + 1) * P], ident[:])
-
-        def scales(t):
-            target = us_ts[t][:] if t < 3 else right[:, t, :]
-            nc.scalar.activation(target, us_sb[:], ACT.Copy, scale=ts_col[:, t:t + 1])
-
         def logits(t):
-            nc.vector.scalar_tensor_tensor(z[t][:], scores[t][:], ts_col[:, t:t + 1], us_sb[:], ALU.mult, ALU.mult)
+            nc.vector.scalar_tensor_tensor(z[t][:], scores[t][:], column(ts_col, t), us_sb[:], ALU.mult, ALU.mult)
 
-        def softmax_numerator(t):
+        def exponentials(t):
             nc.vector.tensor_reduce(neg_max[t][:], z[t][:], AX.X, ALU.max, negate=True)
             nc.scalar.activation(e[t][:], z[t][:], ACT.Exp, bias=neg_max[t][:], accum_out=column(tot, t))
 
-        def scaled_numerator(t):
-            nc.gpsimd.tensor_tensor(right[:, t, :], e[t][:], us_ts[t][:], ALU.mult)
-
-        def recip(first, end):
+        def reciprocals(first, end):
             nc.vector.reciprocal(rtot[:, first:end], tot[:, first:end])
 
-        def weighted(t):
+        h_turned = tiles("h_turned", LAST, [P, R], F32)
+        ts_us = tiles("ts_us", LAST, [P, R], F32)
+        neg_eh = tiles("neg_eh", LAST, [P, R], F32)
+        neg_sum = tile("neg_sum", [P, LAST], F32)
+        rtot2 = tile("rtot2", [P, LAST], F32)
+        bias = tile("bias", [P, LAST], F32)
+
+        def h_turn(t):
+            dp_ps = bank("dp_ps%d" % t, "h_ps%d" % t)
+            for b in range(PACK):
+                nc.tensor.transpose(dp_ps[:, block(b)], dp_sb[t][:, block(b)], ident[:])
+            for b in range(PACK):
+                nc.scalar.activation(h_turned[t][:, block(b)], dp_ps[:, block(b)], ACT.Copy, scale=column(wt_col, b))
+
+        def h_turn_back(t):
+            h[t] = bank("h_ps%d" % t)
+            for b in range(PACK):
+                nc.tensor.transpose(h[t][:, block(b)], h_turned[t][:, block(b)], ident[:])
+
+        def squared_reciprocal(t):
+            nc.scalar.activation(column(rtot2, t), column(rtot, t), ACT.Copy, scale=column(rtot, t))
+
+        def row_sum(t):
             nc.vector.scalar_tensor_tensor(
-                ph[t][:], e[t][:], column(rtot, t), h[t][:], ALU.mult, ALU.mult, accum_out=column(mean, t)
+                neg_eh[t][:], e[t][:], -1.0, h[t][:], ALU.mult, ALU.mult, accum_out=column(neg_sum, t)
             )
 
-        def coefficient(first, end):
-            nc.vector.scalar_tensor_tensor(
-                coef[:, first:end], mean[:, first:end], -1.0, rtot[:, first:end], ALU.mult, ALU.mult
-            )
+        def left_on_scalar(t):
+            nc.scalar.activation(column(bias, t), column(neg_sum, t), ACT.Copy, scale=column(rtot2, t))
+            nc.scalar.activation(left[:, t, :], h[t][:], ACT.Identity, bias=column(bias, t), scale=column(rtot, t))
 
-        def centred_on_scalar(t):
-            nc.scalar.activation(left[:, t, :], h[t][:], ACT.Identity, bias=column(coef, t), scale=column(rtot, t))
+        kt_copy_out(0, "q_raw0")
+        kt_quantise(0)
+        h[LAST] = tile("h_last", [P, R], F32, "q_raw0")
+        nc.gpsimd.tensor_tensor(h[LAST][:], dp_sb[LAST][:], wt_sb[:], ALU.mult)
 
-        def centred_on_vector(t):
-            nc.vector.scalar_tensor_tensor(left[:, t, :], e[t][:], column(coef, t), ph[t][:], ALU.mult, ALU.add)
-
-        kt_evacuate(0, "q_raw0")
-        kt_quantise(0, None)
-        gate_on_gpsimd(3, "q_raw0")
         logits(0)
-        gate_turned(0)
-        logits(1)
-        softmax_numerator(0)
-        gate_turned_back(0)
-        gate_turned(1)
-        logits(2)
-        softmax_numerator(1)
-        gate_turned_back(1)
-        gate_turned(2)
-        logits(3)
-        softmax_numerator(2)
-        gate_turned_back(2)
-        softmax_numerator(3)
+        for t in range(LAST):
+            h_turn(t)
+            logits(t + 1)
+            exponentials(t)
+            h_turn_back(t)
+        exponentials(LAST)
         for t in range(PACK):
-            scales(t)
-        for t in range(3):
-            scaled_numerator(t)
+            target = ts_us[t][:] if t < LAST else right[:, LAST, :]
+            nc.scalar.activation(target, us_sb[:], ACT.Copy, scale=column(ts_col, t))
+        for t in range(LAST):
+            nc.gpsimd.tensor_tensor(right[:, t, :], e[t][:], ts_us[t][:], ALU.mult)
         kt_turn(1, "scores0")
-        recip(0, 2)
-        weighted(0)
-        weighted(1)
-        recip(2, 4)
-        coefficient(0, 2)
-        centred_on_scalar(0)
-        centred_on_scalar(1)
-        weighted(2)
-        coefficient(2, 3)
-        centred_on_scalar(2)
-        weighted(3)
-        coefficient(3, 4)
-        centred_on_vector(3)
-        kt_evacuate(1, "z3")
-        kt_quantise(1, None)
+
+        reciprocals(0, 2)
+        squared_reciprocal(0)
+        squared_reciprocal(1)
+        row_sum(0)
+        left_on_scalar(0)
+        row_sum(1)
+        reciprocals(2, PACK)
+        squared_reciprocal(2)
+        left_on_scalar(1)
+        row_sum(2)
+        left_on_scalar(2)
+
+        ph = tile("ph", [P, R], F32)
+        mean = tile("mean", [P, 1], F32)
+        factor = tile("factor", [P, 1], F32)
+        nc.vector.scalar_tensor_tensor(
+            ph[:], e[LAST][:], column(rtot, LAST), h[LAST][:], ALU.mult, ALU.mult, accum_out=mean[:]
+        )
+        nc.vector.scalar_tensor_tensor(factor[:], mean[:], -1.0, column(rtot, LAST), ALU.mult, ALU.mult)
+        nc.vector.scalar_tensor_tensor(left[:, LAST, :], e[LAST][:], factor[:], ph[:], ALU.mult, ALU.add)
+
+        kt_copy_out(1, "bias")
+        kt_quantise(1)
+
+        spare = bank("spare", "scores0")
+        for b in range(WARM_PASSES):
+            nc.tensor.matmul_mx(
+                spare[:], lhsT=k_codes[:, block(b)].bitcast(E4M3), lhsT_scale=k_scales[:, block(b)],
+                rhs=k_codes[:].bitcast(E4M3), rhs_scale=k_scales[:], start=(b == 0), stop=(b == WARM_PASSES - 1),
+            )
 
         g_words = tile("g_words", [P, R, PACK], BF16)
         g_codes = tile("g_codes", [P, R], U32)
@@ -243,9 +241,9 @@ def tile_attend_gslot_q_kernel(tc, qT, kT, dp, us, ts, wt, offs, out):
         for c in range(2):
             cols = slice(c * HALF, (c + 1) * HALF)
             nc.vector.tensor_tensor(
-                g_words[:, cols, :].rearrange("s (c i) t -> s c t i", i=2),
-                left[:, :, cols].rearrange("s t (c i) -> s c t i", i=2),
-                right[:, :, cols].rearrange("s t (c i) -> s c t i", i=2),
+                g_words[:, cols, :].rearrange("s (n x) t -> s n t x", x=2),
+                left[:, :, cols].rearrange("s t (n x) -> s n t x", x=2),
+                right[:, :, cols].rearrange("s t (n x) -> s n t x", x=2),
                 ALU.mult,
             )
         for c in range(2):
@@ -257,14 +255,12 @@ def tile_attend_gslot_q_kernel(tc, qT, kT, dp, us, ts, wt, offs, out):
         out_rows = out.rearrange("(p j) r -> p j r", j=PACK)
         result = tiles("result", PACK, [P, R], F32)
         for j in range(PACK):
+            u, v = divmod(j, 2)
             acc = bank("acc%d" % j, "scores%d" % j)
-            cols = slice(j % 2 * P, (j % 2 + 1) * P)
             nc.tensor.matmul_mx(
-                acc[:], lhsT=kt_codes[j // 2][:, cols].bitcast(E4M3), lhsT_scale=kt_scales[j // 2][:, cols],
+                acc[:], lhsT=kt_codes[u][:, block(v)].bitcast(E4M3), lhsT_scale=kt_scales[u][:, block(v)],
                 rhs=g_codes[:].bitcast(E5M2), rhs_scale=g_scales[:], start=True, stop=True,
             )
-            if j % 2 == 0:
-                nc.scalar.copy(result[j][:], acc[:])
-            else:
-                nc.vector.tensor_copy(result[j][:], acc[:])
+            copy = nc.scalar.copy if v == 0 else nc.vector.tensor_copy
+            copy(result[j][:], acc[:])
             nc.sync.dma_start(out_rows[:, j, :], result[j][:])

@@ -19,7 +19,8 @@ PACK = 4
 D, R, SLOTS, TOKENS = 512, 512, 512, 2048
 HALF = R // 2
 LAST = PACK - 1
-WARM_PASSES = 2
+EARLY = 128
+REST = R - EARLY
 FLOPS = 2 * 2 * D * R * SLOTS
 
 
@@ -228,39 +229,48 @@ def tile_attend_gslot_q_kernel(tc, qT, kT, dp, us, ts, wt, offs, out):
         kt_copy_out(1, "bias")
         kt_quantise(1)
 
-        spare = bank("spare", "scores0")
-        for b in range(WARM_PASSES):
-            nc.tensor.matmul_mx(
-                spare[:], lhsT=k_codes[:, block(b)].bitcast(E4M3), lhsT_scale=k_scales[:, block(b)],
-                rhs=k_codes[:].bitcast(E4M3), rhs_scale=k_scales[:], start=(b == 0), stop=(b == WARM_PASSES - 1),
-            )
-
         g_words = tile("g_words", [P, R, PACK], BF16)
-        g_codes = tile("g_codes", [P, R], U32)
-        g_scales = tile("g_scales", [P, R], U8)
-        for c in range(2):
-            cols = slice(c * HALF, (c + 1) * HALF)
+        g_codes = tile("g_codes", [P, REST + R], U32)
+        g_scales = tile("g_scales", [P, REST + R], U8)
+        nc.gpsimd.memset(g_codes[:, 0:REST], 0)
+        nc.gpsimd.memset(g_scales[:, 0:REST], 0)
+        out_rows = out.rearrange("(p j) r -> p j r", j=PACK)
+
+        def g_form(first, end):
             nc.vector.tensor_tensor(
-                g_words[:, cols, :].rearrange("s (n x) t -> s n t x", x=2),
-                left[:, :, cols].rearrange("s t (n x) -> s n t x", x=2),
-                right[:, :, cols].rearrange("s t (n x) -> s n t x", x=2),
+                g_words[:, first:end, :].rearrange("s (n x) t -> s n t x", x=2),
+                left[:, :, first:end].rearrange("s t (n x) -> s n t x", x=2),
+                right[:, :, first:end].rearrange("s t (n x) -> s n t x", x=2),
                 ALU.mult,
             )
-        for c in range(2):
-            cols = slice(c * HALF, (c + 1) * HALF)
+
+        def g_quantise(first, end):
+            cols = slice(REST + first, REST + end)
             nc.vector.quantize_mx(
-                g_codes[:, cols].bitcast(E5M2), g_scales[:, cols], g_words[:, cols, :].rearrange("s r t -> s (r t)")
+                g_codes[:, cols].bitcast(E5M2), g_scales[:, cols], g_words[:, first:end, :].rearrange("s r t -> s (r t)")
             )
 
-        out_rows = out.rearrange("(p j) r -> p j r", j=PACK)
-        result = tiles("result", PACK, [P, R], F32)
-        for j in range(PACK):
-            u, v = divmod(j, 2)
-            acc = bank("acc%d" % j, "scores%d" % j)
+        def product(name, j, window, cuts, on, copy):
+            acc = bank(name, on)
+            cols = slice(window, window + R)
             nc.tensor.matmul_mx(
-                acc[:], lhsT=kt_codes[u][:, block(v)].bitcast(E4M3), lhsT_scale=kt_scales[u][:, block(v)],
-                rhs=g_codes[:].bitcast(E5M2), rhs_scale=g_scales[:], start=True, stop=True,
+                acc[:], lhsT=kt_codes[j // 2][:, block(j % 2)].bitcast(E4M3), lhsT_scale=kt_scales[j // 2][:, block(j % 2)],
+                rhs=g_codes[:, cols].bitcast(E5M2), rhs_scale=g_scales[:, cols], start=True, stop=True,
             )
-            copy = nc.scalar.copy if v == 0 else nc.vector.tensor_copy
-            copy(result[j][:], acc[:])
-            nc.sync.dma_start(out_rows[:, j, :], result[j][:])
+            for first, end in zip(cuts, cuts[1:]):
+                result = tile("%s_sb%d" % (name, first), [P, end - first], F32)
+                copy(result[:], acc[:, REST - window + first:REST - window + end])
+                nc.sync.dma_start(out_rows[:, j, first:end], result[:])
+
+        g_form(0, EARLY)
+        g_form(EARLY, EARLY + P)
+        g_quantise(0, EARLY)
+        for j in range(2):
+            product("early%d" % j, j, 0, (0, EARLY), "scores%d" % (j + 1), nc.scalar.copy)
+        g_form(HALF, R)
+        g_quantise(EARLY, HALF)
+        g_quantise(HALF, R)
+        product("late2", 2, REST, (0, HALF, R), "scores0", nc.scalar.copy)
+        product("late3", 3, REST, (0, R), "scores3", nc.vector.tensor_copy)
+        product("late0", 0, REST, (EARLY, R), "h_ps0", nc.scalar.copy)
+        product("late1", 1, REST, (EARLY, R), "h_ps1", nc.vector.tensor_copy)

@@ -69,7 +69,7 @@ def tile_attend_gslot_q_kernel(tc, qT, kT, dp, us, ts, wt, offs, out):
         dp_rows = dp.rearrange("(s t) r -> s t r", t=PACK)
         nc.sync.dma_start(us_sb[:], us)
         nc.sync.dma_start(wt_sb[:], wt)
-        for t in range(PACK):
+        for t in (LAST, 0, 1, 2):
             nc.sync.dma_start(dp_sb[t][:], dp_rows[:, t, :])
 
         ident = tile("ident", [P, P], F32)
@@ -99,7 +99,7 @@ def tile_attend_gslot_q_kernel(tc, qT, kT, dp, us, ts, wt, offs, out):
 
         k_pairs = k_words[:].rearrange("p t s j -> p (t s j)").bitcast(F32).rearrange("p (t s u) -> p t s u", t=PACK, u=2)
         kt_ps, kt_words = {}, {}
-        kt_codes = tiles("kt_codes", 2, [P, 2 * P], U32)
+        kt_codes = {}
         kt_scales = tiles("kt_scales", 2, [P, 2 * P], U8)
 
         def kt_turn(u, on):
@@ -111,7 +111,8 @@ def tile_attend_gslot_q_kernel(tc, qT, kT, dp, us, ts, wt, offs, out):
             kt_words[u] = tile("kt_words%d" % u, [P, 2, P, PACK], BF16, on)
             nc.scalar.copy(kt_words[u][:], kt_ps[u][:].bitcast(BF16).rearrange("s (t p v) -> s v p t", t=PACK, v=2))
 
-        def kt_quantise(u):
+        def kt_quantise(u, on):
+            kt_codes[u] = tile("kt_codes%d" % u, [P, 2 * P], U32, on)
             nc.vector.quantize_mx(
                 kt_codes[u][:].bitcast(E4M3), kt_scales[u][:], kt_words[u][:].rearrange("s v p t -> s (v p t)")
             )
@@ -119,8 +120,8 @@ def tile_attend_gslot_q_kernel(tc, qT, kT, dp, us, ts, wt, offs, out):
         kt_turn(0, None)
 
         q_words = tiles("q_words", 2, [P, HALF, PACK], BF16)
-        q_codes = tiles("q_codes", 2, [P, HALF], U32)
-        q_scales = tiles("q_scales", 2, [P, HALF], U8)
+        q_codes = tile("q_codes", [P, R], U32)
+        q_scales = tile("q_scales", [P, R], U8)
         for c, copy in enumerate((nc.scalar.copy, nc.vector.tensor_copy)):
             copy(
                 q_words[c][:].rearrange("p (n x) j -> p n j x", x=4),
@@ -128,25 +129,34 @@ def tile_attend_gslot_q_kernel(tc, qT, kT, dp, us, ts, wt, offs, out):
             )
         scores = [bank("scores%d" % t) for t in range(PACK)]
         for c in range(2):
-            nc.vector.quantize_mx(q_codes[c][:].bitcast(E4M3), q_scales[c][:], q_words[c][:].rearrange("p r j -> p (r j)"))
-            for t in range(PACK):
-                nc.tensor.matmul_mx(
-                    scores[t][:, c * HALF:(c + 1) * HALF],
-                    lhsT=k_codes[:, block(t)].bitcast(E4M3), lhsT_scale=k_scales[:, block(t)],
-                    rhs=q_codes[c][:].bitcast(E4M3), rhs_scale=q_scales[c][:], start=True, stop=True,
-                )
+            cols = slice(c * HALF, (c + 1) * HALF)
+            nc.vector.quantize_mx(q_codes[:, cols].bitcast(E4M3), q_scales[:, cols], q_words[c][:].rearrange("p r j -> p (r j)"))
+
+        def score(target, t, first, end):
+            nc.tensor.matmul_mx(
+                target[:, first:end], lhsT=k_codes[:, block(t)].bitcast(E4M3), lhsT_scale=k_scales[:, block(t)],
+                rhs=q_codes[:, first:end].bitcast(E4M3), rhs_scale=q_scales[:, first:end], start=True, stop=True,
+            )
+
+        head = bank("scores_head", "h_ps2")
+        score(head, 0, 0, HALF)
+        score(scores[0], 0, HALF, R)
+        for t in range(1, PACK):
+            score(scores[t], t, 0, R)
 
         z = tiles("z", PACK, [P, R], F32)
         e = tiles("e", PACK, [P, R], F32)
         neg_max = tiles("neg_max", PACK, [P, 1], F32)
         tot = tile("tot", [P, PACK], F32)
         rtot = tile("rtot", [P, PACK], F32)
-        left = tile("left", [P, PACK, R], F32)
+        left = tiles("left", 2, [P, PACK, HALF], F32)
         right = tile("right", [P, PACK, R], F32)
         h = {}
 
-        def logits(t):
-            nc.vector.scalar_tensor_tensor(z[t][:], scores[t][:], column(ts_col, t), us_sb[:], ALU.mult, ALU.mult)
+        def logits(t, source, first, end):
+            nc.vector.scalar_tensor_tensor(
+                z[t][:, first:end], source[:, first:end], column(ts_col, t), us_sb[:, first:end], ALU.mult, ALU.mult
+            )
 
         def exponentials(t):
             nc.vector.tensor_reduce(neg_max[t][:], z[t][:], AX.X, ALU.max, negate=True)
@@ -156,7 +166,7 @@ def tile_attend_gslot_q_kernel(tc, qT, kT, dp, us, ts, wt, offs, out):
             nc.vector.reciprocal(rtot[:, first:end], tot[:, first:end])
 
         h_turned = tiles("h_turned", LAST, [P, R], F32)
-        ts_us = tiles("ts_us", LAST, [P, R], F32)
+        ts_us = tiles("ts_us", PACK, [P, R], F32)
         neg_eh = tiles("neg_eh", LAST, [P, R], F32)
         neg_sum = tile("neg_sum", [P, LAST], F32)
         rtot2 = tile("rtot2", [P, LAST], F32)
@@ -182,25 +192,34 @@ def tile_attend_gslot_q_kernel(tc, qT, kT, dp, us, ts, wt, offs, out):
                 neg_eh[t][:], e[t][:], -1.0, h[t][:], ALU.mult, ALU.mult, accum_out=column(neg_sum, t)
             )
 
-        def left_on_scalar(t):
+        def centre(t):
             nc.scalar.activation(column(bias, t), column(neg_sum, t), ACT.Copy, scale=column(rtot2, t))
-            nc.scalar.activation(left[:, t, :], h[t][:], ACT.Identity, bias=column(bias, t), scale=column(rtot, t))
+
+        def left_on_scalar(t, c):
+            nc.scalar.activation(
+                left[c][:, t, :], h[t][:, c * HALF:(c + 1) * HALF], ACT.Identity, bias=column(bias, t), scale=column(rtot, t)
+            )
 
         kt_copy_out(0, "q_raw0")
-        kt_quantise(0)
+        kt_quantise(0, None)
         h[LAST] = tile("h_last", [P, R], F32, "q_raw0")
         nc.gpsimd.tensor_tensor(h[LAST][:], dp_sb[LAST][:], wt_sb[:], ALU.mult)
 
-        logits(0)
-        for t in range(LAST):
-            h_turn(t)
-            logits(t + 1)
+        logits(0, head, 0, HALF)
+        logits(0, scores[0], HALF, R)
+        logits(1, scores[1], 0, HALF)
+        exponentials(0)
+        h_turn(0)
+        logits(1, scores[1], HALF, R)
+        h_turn_back(0)
+        for t in range(1, LAST):
+            logits(t + 1, scores[t + 1], 0, R)
             exponentials(t)
+            h_turn(t)
             h_turn_back(t)
         exponentials(LAST)
         for t in range(PACK):
-            target = ts_us[t][:] if t < LAST else right[:, LAST, :]
-            nc.scalar.activation(target, us_sb[:], ACT.Copy, scale=column(ts_col, t))
+            nc.scalar.activation(ts_us[t][:], us_sb[:], ACT.Copy, scale=column(ts_col, t))
         for t in range(LAST):
             nc.gpsimd.tensor_tensor(right[:, t, :], e[t][:], ts_us[t][:], ALU.mult)
         kt_turn(1, "scores0")
@@ -209,25 +228,33 @@ def tile_attend_gslot_q_kernel(tc, qT, kT, dp, us, ts, wt, offs, out):
         squared_reciprocal(0)
         squared_reciprocal(1)
         row_sum(0)
-        left_on_scalar(0)
+        centre(0)
+        left_on_scalar(0, 0)
+        left_on_scalar(0, 1)
         row_sum(1)
         reciprocals(2, PACK)
         squared_reciprocal(2)
-        left_on_scalar(1)
+        centre(1)
+        left_on_scalar(1, 0)
         row_sum(2)
-        left_on_scalar(2)
+        centre(2)
+        left_on_scalar(2, 0)
+        left_on_scalar(1, 1)
+        left_on_scalar(2, 1)
 
         ph = tile("ph", [P, R], F32)
         mean = tile("mean", [P, 1], F32)
-        factor = tile("factor", [P, 1], F32)
         nc.vector.scalar_tensor_tensor(
             ph[:], e[LAST][:], column(rtot, LAST), h[LAST][:], ALU.mult, ALU.mult, accum_out=mean[:]
         )
-        nc.vector.scalar_tensor_tensor(factor[:], mean[:], -1.0, column(rtot, LAST), ALU.mult, ALU.mult)
-        nc.vector.scalar_tensor_tensor(left[:, LAST, :], e[LAST][:], factor[:], ph[:], ALU.mult, ALU.add)
+        nc.vector.tensor_scalar(right[:, LAST, :], ts_us[LAST][:], column(rtot, LAST), None, ALU.mult)
+        for c in range(2):
+            cols = slice(c * HALF, (c + 1) * HALF)
+            nc.vector.scalar_tensor_tensor(
+                left[c][:, LAST, :], h[LAST][:, cols], mean[:], e[LAST][:, cols], ALU.subtract, ALU.mult
+            )
 
         kt_copy_out(1, "bias")
-        kt_quantise(1)
 
         g_words = tile("g_words", [P, R, PACK], BF16)
         g_codes = tile("g_codes", [P, REST + R], U32)
@@ -239,7 +266,7 @@ def tile_attend_gslot_q_kernel(tc, qT, kT, dp, us, ts, wt, offs, out):
         def g_form(first, end):
             nc.vector.tensor_tensor(
                 g_words[:, first:end, :].rearrange("s (n x) t -> s n t x", x=2),
-                left[:, :, first:end].rearrange("s t (n x) -> s n t x", x=2),
+                left[first // HALF][:, :, first % HALF:first % HALF + end - first].rearrange("s t (n x) -> s n t x", x=2),
                 right[:, :, first:end].rearrange("s t (n x) -> s n t x", x=2),
                 ALU.mult,
             )
@@ -270,7 +297,8 @@ def tile_attend_gslot_q_kernel(tc, qT, kT, dp, us, ts, wt, offs, out):
         g_form(HALF, R)
         g_quantise(EARLY, HALF)
         g_quantise(HALF, R)
-        product("late2", 2, REST, (0, HALF, R), "scores0", nc.scalar.copy)
-        product("late3", 3, REST, (0, R), "scores3", nc.vector.tensor_copy)
-        product("late0", 0, REST, (EARLY, R), "h_ps0", nc.scalar.copy)
+        kt_quantise(1, "g_words")
+        product("late0", 0, REST, (EARLY, HALF, R), "h_ps0", nc.scalar.copy)
         product("late1", 1, REST, (EARLY, R), "h_ps1", nc.vector.tensor_copy)
+        product("late2", 2, REST, (0, R), "scores0", nc.scalar.copy)
+        product("late3", 3, REST, (0, R), "scores3", nc.vector.tensor_copy)

@@ -69,11 +69,13 @@ def tile_attend_gslot_q_kernel(tc, qT, kT, dp, us, ts, wt, offs, out):
         dp_rows = dp.rearrange("(s t) r -> s t r", t=PACK)
         nc.sync.dma_start(us_sb[:], us)
         nc.sync.dma_start(wt_sb[:], wt)
-        for t in (LAST, 0, 1, 2):
+        for t in (0, LAST, 1, 2):
             nc.sync.dma_start(dp_sb[t][:], dp_rows[:, t, :])
 
         ident = tile("ident", [P, P], F32)
         make_identity(nc, ident[:])
+        ident16 = tile("ident16", [P, P], BF16)
+        make_identity(nc, ident16[:])
 
         def to_columns(name, blocks, on):
             turned = bank(name + "_ps", on)
@@ -89,18 +91,35 @@ def tile_attend_gslot_q_kernel(tc, qT, kT, dp, us, ts, wt, offs, out):
         wt_col = to_columns("wt_col", [wt_row[:, block(b)] for b in range(PACK)], "h_ps1")
 
         k_words = tile("k_words", [P, PACK, P, PACK], BF16)
-        for j in range(PACK):
+        kt_ps, kt_words, kt_codes = {}, {}, {}
+        kt_scales = tiles("kt_scales", 2, [P, 2 * P], U8)
+
+        def k_gather(j):
             nc.vector.tensor_copy(
                 k_words[:, :, :, j].rearrange("p t s -> p s t"), k_plane[j][:].indirect(offsets[:])
             )
+
+        def kt_quantise(u, on):
+            kt_codes[u] = tile("kt_codes%d" % u, [P, 2 * P], U32, on)
+            nc.vector.quantize_mx(
+                kt_codes[u][:].bitcast(E4M3), kt_scales[u][:], kt_words[u][:].rearrange("s v p t -> s (v p t)")
+            )
+
+        kt_words[0] = tile("kt_words0", [P, 2, P, PACK], BF16)
+        for j in range(2):
+            k_gather(j)
+            turned = ps.tile([P, 2 * R], BF16, name="kt_plane%d" % j, tag="scores%d" % j)
+            for t in range(PACK):
+                nc.tensor.transpose(turned[:, block(t)], k_words[:, t, :, j], ident16[:])
+            nc.scalar.copy(kt_words[0][:, j, :, :], turned[:, 0:R].rearrange("s (t p) -> s p t", t=PACK))
+        for j in range(2, PACK):
+            k_gather(j)
+        kt_quantise(0, "k_plane%d" % LAST)
         k_codes = tile("k_codes", [P, SLOTS], U32)
         k_scales = tile("k_scales", [P, SLOTS], U8)
         nc.vector.quantize_mx(k_codes[:].bitcast(E4M3), k_scales[:], k_words[:].rearrange("p t s j -> p (t s j)"))
 
         k_pairs = k_words[:].rearrange("p t s j -> p (t s j)").bitcast(F32).rearrange("p (t s u) -> p t s u", t=PACK, u=2)
-        kt_ps, kt_words = {}, {}
-        kt_codes = {}
-        kt_scales = tiles("kt_scales", 2, [P, 2 * P], U8)
 
         def kt_turn(u, on):
             kt_ps[u] = bank("kt_ps%d" % u, on)
@@ -111,13 +130,7 @@ def tile_attend_gslot_q_kernel(tc, qT, kT, dp, us, ts, wt, offs, out):
             kt_words[u] = tile("kt_words%d" % u, [P, 2, P, PACK], BF16, on)
             nc.scalar.copy(kt_words[u][:], kt_ps[u][:].bitcast(BF16).rearrange("s (t p v) -> s v p t", t=PACK, v=2))
 
-        def kt_quantise(u, on):
-            kt_codes[u] = tile("kt_codes%d" % u, [P, 2 * P], U32, on)
-            nc.vector.quantize_mx(
-                kt_codes[u][:].bitcast(E4M3), kt_scales[u][:], kt_words[u][:].rearrange("s v p t -> s (v p t)")
-            )
-
-        kt_turn(0, None)
+        kt_turn(1, None)
 
         q_words = tiles("q_words", 2, [P, HALF, PACK], BF16)
         q_codes = tile("q_codes", [P, R], U32)
@@ -141,8 +154,19 @@ def tile_attend_gslot_q_kernel(tc, qT, kT, dp, us, ts, wt, offs, out):
         head = bank("scores_head", "h_ps2")
         score(head, 0, 0, HALF)
         score(scores[0], 0, HALF, R)
-        for t in range(1, PACK):
-            score(scores[t], t, 0, R)
+        dp_ps = {}
+
+        def dp_turn(t):
+            dp_ps[t] = bank("dp_ps%d" % t, "h_ps%d" % t)
+            for b in range(PACK):
+                nc.tensor.transpose(dp_ps[t][:, block(b)], dp_sb[t][:, block(b)], ident[:])
+
+        score(scores[1], 1, 0, R)
+        dp_turn(0)
+        score(scores[2], 2, 0, R)
+        score(scores[3], 3, 0, R)
+        dp_turn(1)
+        dp_turn(2)
 
         z = tiles("z", PACK, [P, R], F32)
         e = tiles("e", PACK, [P, R], F32)
@@ -173,11 +197,8 @@ def tile_attend_gslot_q_kernel(tc, qT, kT, dp, us, ts, wt, offs, out):
         bias = tile("bias", [P, LAST], F32)
 
         def h_turn(t):
-            dp_ps = bank("dp_ps%d" % t, "h_ps%d" % t)
             for b in range(PACK):
-                nc.tensor.transpose(dp_ps[:, block(b)], dp_sb[t][:, block(b)], ident[:])
-            for b in range(PACK):
-                nc.scalar.activation(h_turned[t][:, block(b)], dp_ps[:, block(b)], ACT.Copy, scale=column(wt_col, b))
+                nc.scalar.activation(h_turned[t][:, block(b)], dp_ps[t][:, block(b)], ACT.Copy, scale=column(wt_col, b))
 
         def h_turn_back(t):
             h[t] = bank("h_ps%d" % t)
@@ -200,9 +221,7 @@ def tile_attend_gslot_q_kernel(tc, qT, kT, dp, us, ts, wt, offs, out):
                 left[c][:, t, :], h[t][:, c * HALF:(c + 1) * HALF], ACT.Identity, bias=column(bias, t), scale=column(rtot, t)
             )
 
-        kt_copy_out(0, "q_raw0")
-        kt_quantise(0, None)
-        h[LAST] = tile("h_last", [P, R], F32, "q_raw0")
+        h[LAST] = tile("h_last", [P, R], F32, "q_words1")
         nc.gpsimd.tensor_tensor(h[LAST][:], dp_sb[LAST][:], wt_sb[:], ALU.mult)
 
         logits(0, head, 0, HALF)
@@ -222,7 +241,6 @@ def tile_attend_gslot_q_kernel(tc, qT, kT, dp, us, ts, wt, offs, out):
             nc.scalar.activation(ts_us[t][:], us_sb[:], ACT.Copy, scale=column(ts_col, t))
         for t in range(LAST):
             nc.gpsimd.tensor_tensor(right[:, t, :], e[t][:], ts_us[t][:], ALU.mult)
-        kt_turn(1, "scores0")
 
         reciprocals(0, 2)
         squared_reciprocal(0)
@@ -301,4 +319,4 @@ def tile_attend_gslot_q_kernel(tc, qT, kT, dp, us, ts, wt, offs, out):
         product("late0", 0, REST, (EARLY, HALF, R), "h_ps0", nc.scalar.copy)
         product("late1", 1, REST, (EARLY, R), "h_ps1", nc.vector.tensor_copy)
         product("late2", 2, REST, (0, R), "scores0", nc.scalar.copy)
-        product("late3", 3, REST, (0, R), "scores3", nc.vector.tensor_copy)
+        product("late3", 3, REST, (0, HALF, R), "scores3", nc.vector.tensor_copy)

@@ -19,8 +19,6 @@ PACK = 4
 D, R, SLOTS, TOKENS = 512, 512, 512, 2048
 HALF = R // 2
 LAST = PACK - 1
-EARLY = 128
-REST = R - EARLY
 FLOPS = 2 * 2 * D * R * SLOTS
 
 
@@ -274,49 +272,47 @@ def tile_attend_gslot_q_kernel(tc, qT, kT, dp, us, ts, wt, offs, out):
 
         kt_copy_out(1, "bias")
 
-        g_words = tile("g_words", [P, R, PACK], BF16)
-        g_codes = tile("g_codes", [P, REST + R], U32)
-        g_scales = tile("g_scales", [P, REST + R], U8)
-        nc.gpsimd.memset(g_codes[:, 0:REST], 0)
-        nc.gpsimd.memset(g_scales[:, 0:REST], 0)
         out_rows = out.rearrange("(p j) r -> p j r", j=PACK)
+        g_words, g_codes, g_scales = {}, {}, {}
 
-        def g_form(first, end):
+        def g_form(x):
+            first = x * P
+            g_words[x] = tile("g_words%d" % x, [P, P, PACK], BF16, "g_words%d" % (x % 2))
             nc.vector.tensor_tensor(
-                g_words[:, first:end, :].rearrange("s (n x) t -> s n t x", x=2),
-                left[first // HALF][:, :, first % HALF:first % HALF + end - first].rearrange("s t (n x) -> s n t x", x=2),
-                right[:, :, first:end].rearrange("s t (n x) -> s n t x", x=2),
+                g_words[x][:].rearrange("s (n x) t -> s n t x", x=2),
+                left[first // HALF][:, :, first % HALF:first % HALF + P].rearrange("s t (n x) -> s n t x", x=2),
+                right[:, :, first:first + P].rearrange("s t (n x) -> s n t x", x=2),
                 ALU.mult,
             )
 
-        def g_quantise(first, end):
-            cols = slice(REST + first, REST + end)
-            nc.vector.quantize_mx(
-                g_codes[:, cols].bitcast(E5M2), g_scales[:, cols], g_words[:, first:end, :].rearrange("s r t -> s (r t)")
-            )
+        def g_quantise(x):
+            g_codes[x] = tile("g_codes%d" % x, [P, P], U32)
+            g_scales[x] = tile("g_scales%d" % x, [P, P], U8)
+            nc.vector.quantize_mx(g_codes[x][:].bitcast(E5M2), g_scales[x][:], g_words[x][:].rearrange("s r t -> s (r t)"))
 
-        def product(name, j, window, cuts, on, copy):
-            acc = bank(name, on)
-            cols = slice(window, window + R)
-            nc.tensor.matmul_mx(
-                acc[:], lhsT=kt_codes[j // 2][:, block(j % 2)].bitcast(E4M3), lhsT_scale=kt_scales[j // 2][:, block(j % 2)],
-                rhs=g_codes[:, cols].bitcast(E5M2), rhs_scale=g_scales[:, cols], start=True, stop=True,
-            )
-            for first, end in zip(cuts, cuts[1:]):
-                result = tile("%s_sb%d" % (name, first), [P, end - first], F32)
-                copy(result[:], acc[:, REST - window + first:REST - window + end])
-                nc.sync.dma_start(out_rows[:, j, first:end], result[:])
+        def product(x, first, end, on, copy):
+            acc = bank("acc%d_%d" % (x, first), on)
+            for j in range(first, end):
+                nc.tensor.matmul_mx(
+                    acc[:, block(j - first)], lhsT=kt_codes[j // 2][:, block(j % 2)].bitcast(E4M3),
+                    lhsT_scale=kt_scales[j // 2][:, block(j % 2)],
+                    rhs=g_codes[x][:].bitcast(E5M2), rhs_scale=g_scales[x][:], start=True, stop=True,
+                )
+            result = tile("result%d_%d" % (x, first), [P, end - first, P], F32)
+            copy(result[:].rearrange("p j r -> p (j r)"), acc[:, 0:(end - first) * P])
+            nc.sync.dma_start(out_rows[:, first:end, block(x)], result[:])
 
-        g_form(0, EARLY)
-        g_form(EARLY, EARLY + P)
-        g_quantise(0, EARLY)
-        for j in range(2):
-            product("early%d" % j, j, 0, (0, EARLY), "scores%d" % (j + 1), nc.scalar.copy)
-        g_form(HALF, R)
-        g_quantise(EARLY, HALF)
-        g_quantise(HALF, R)
-        kt_quantise(1, "g_words")
-        product("late0", 0, REST, (EARLY, HALF, R), "h_ps0", nc.scalar.copy)
-        product("late1", 1, REST, (EARLY, R), "h_ps1", nc.vector.tensor_copy)
-        product("late2", 2, REST, (0, R), "scores0", nc.scalar.copy)
-        product("late3", 3, REST, (0, HALF, R), "scores3", nc.vector.tensor_copy)
+        g_form(0)
+        g_form(1)
+        g_quantise(0)
+        kt_quantise(1, "neg_eh2")
+        product(0, 0, PACK, "scores0", nc.scalar.copy)
+        g_form(2)
+        g_quantise(1)
+        product(1, 0, PACK, "scores1", nc.scalar.copy)
+        g_form(3)
+        g_quantise(2)
+        product(2, 0, PACK, "scores2", nc.scalar.copy)
+        g_quantise(3)
+        product(3, 0, 2, "scores3", nc.vector.tensor_copy)
+        product(3, 2, PACK, "h_ps0", nc.scalar.copy)

@@ -89,46 +89,34 @@ def tile_attend_gslot_q_kernel(tc, qT, kT, dp, us, ts, wt, offs, out):
         wt_col = to_columns("wt_col", [wt_row[:, block(b)] for b in range(PACK)], "h_ps1")
 
         k_words = tile("k_words", [P, PACK, P, PACK], BF16)
-        kt_ps, kt_words, kt_codes = {}, {}, {}
         kt_scales = tiles("kt_scales", 2, [P, 2 * P], U8)
+        kt_codes = {}
 
         def k_gather(j):
             nc.vector.tensor_copy(
                 k_words[:, :, :, j].rearrange("p t s -> p s t"), k_plane[j][:].indirect(offsets[:])
             )
 
-        def kt_quantise(u, on):
-            kt_codes[u] = tile("kt_codes%d" % u, [P, 2 * P], U32, on)
-            nc.vector.quantize_mx(
-                kt_codes[u][:].bitcast(E4M3), kt_scales[u][:], kt_words[u][:].rearrange("s v p t -> s (v p t)")
-            )
-
-        kt_words[0] = tile("kt_words0", [P, 2, P, PACK], BF16)
-        for j in range(2):
-            k_gather(j)
-            turned = ps.tile([P, 2 * R], BF16, name="kt_plane%d" % j, tag="scores%d" % j)
+        def kt_turn(j, on):
+            turned = ps.tile([P, 2 * R], BF16, name="kt_plane%d" % j, tag=on)
             for t in range(PACK):
                 nc.tensor.transpose(turned[:, block(t)], k_words[:, t, :, j], ident16[:])
-            nc.scalar.copy(kt_words[0][:, j, :, :], turned[:, 0:R].rearrange("s (t p) -> s p t", t=PACK))
-        for j in range(2, PACK):
+            return turned[:, 0:R].rearrange("s (t p) -> s p t", t=PACK)
+
+        kt_pair = tile("kt_pair", [P, 2, P, PACK], BF16)
+        for j in range(2):
             k_gather(j)
-        kt_quantise(0, "k_plane%d" % LAST)
+            nc.scalar.copy(kt_pair[:, j, :, :], kt_turn(j, "scores%d" % j))
+        k_gather(2)
+        kt_codes[0] = tile("kt_codes0", [P, 2 * P], U32, "k_plane2")
+        nc.vector.quantize_mx(kt_codes[0][:].bitcast(E4M3), kt_scales[0][:], kt_pair[:].rearrange("s v p t -> s (v p t)"))
+        kt_third = tile("kt_third", [P, P, PACK], BF16)
+        nc.scalar.copy(kt_third[:], kt_turn(2, "scores2"))
+        k_gather(LAST)
+        kt_last_ps = kt_turn(LAST, "kt_last_ps")
         k_codes = tile("k_codes", [P, SLOTS], U32)
         k_scales = tile("k_scales", [P, SLOTS], U8)
         nc.vector.quantize_mx(k_codes[:].bitcast(E4M3), k_scales[:], k_words[:].rearrange("p t s j -> p (t s j)"))
-
-        k_pairs = k_words[:].rearrange("p t s j -> p (t s j)").bitcast(F32).rearrange("p (t s u) -> p t s u", t=PACK, u=2)
-
-        def kt_turn(u, on):
-            kt_ps[u] = bank("kt_ps%d" % u, on)
-            for t in range(PACK):
-                nc.tensor.transpose(kt_ps[u][:, block(t)], k_pairs[:, t, :, u], ident[:])
-
-        def kt_copy_out(u, on):
-            kt_words[u] = tile("kt_words%d" % u, [P, 2, P, PACK], BF16, on)
-            nc.scalar.copy(kt_words[u][:], kt_ps[u][:].bitcast(BF16).rearrange("s (t p v) -> s v p t", t=PACK, v=2))
-
-        kt_turn(1, None)
 
         q_words = tiles("q_words", 2, [P, HALF, PACK], BF16)
         q_codes = tile("q_codes", [P, R], U32)
@@ -138,10 +126,17 @@ def tile_attend_gslot_q_kernel(tc, qT, kT, dp, us, ts, wt, offs, out):
                 q_words[c][:].rearrange("p (n x) j -> p n j x", x=4),
                 q_raw[c][:].rearrange("p j (n x) -> p n j x", x=4),
             )
+        kt_last = tile("kt_last", [P, P, PACK], BF16, "q_raw0")
+        nc.scalar.copy(kt_last[:], kt_last_ps)
         scores = [bank("scores%d" % t) for t in range(PACK)]
         for c in range(2):
             cols = slice(c * HALF, (c + 1) * HALF)
             nc.vector.quantize_mx(q_codes[:, cols].bitcast(E4M3), q_scales[:, cols], q_words[c][:].rearrange("p r j -> p (r j)"))
+        kt_codes[1] = tile("kt_codes1", [P, 2 * P], U32, "q_words0")
+        for v, words in enumerate((kt_third, kt_last)):
+            nc.vector.quantize_mx(
+                kt_codes[1][:, block(v)].bitcast(E4M3), kt_scales[1][:, block(v)], words[:].rearrange("s p t -> s (p t)")
+            )
 
         def score(target, t, first, end):
             nc.tensor.matmul_mx(
@@ -270,18 +265,18 @@ def tile_attend_gslot_q_kernel(tc, qT, kT, dp, us, ts, wt, offs, out):
                 left[c][:, LAST, :], h[LAST][:, cols], mean[:], e[LAST][:, cols], ALU.subtract, ALU.mult
             )
 
-        kt_copy_out(1, "bias")
 
         out_rows = out.rearrange("(p j) r -> p j r", j=PACK)
         g_words, g_codes, g_scales = {}, {}, {}
 
-        def g_form(x):
-            first = x * P
-            g_words[x] = tile("g_words%d" % x, [P, P, PACK], BF16, "g_words%d" % (x % 2))
+        def g_form(x, start=0, stop=P):
+            first, end = x * P + start, x * P + stop
+            if start == 0:
+                g_words[x] = tile("g_words%d" % x, [P, P, PACK], BF16, "g_words%d" % (x % 2))
             nc.vector.tensor_tensor(
-                g_words[x][:].rearrange("s (n x) t -> s n t x", x=2),
-                left[first // HALF][:, :, first % HALF:first % HALF + P].rearrange("s t (n x) -> s n t x", x=2),
-                right[:, :, first:first + P].rearrange("s t (n x) -> s n t x", x=2),
+                g_words[x][:, start:stop, :].rearrange("s (n x) t -> s n t x", x=2),
+                left[first // HALF][:, :, first % HALF:first % HALF + end - first].rearrange("s t (n x) -> s n t x", x=2),
+                right[:, :, first:end].rearrange("s t (n x) -> s n t x", x=2),
                 ALU.mult,
             )
 
@@ -303,16 +298,11 @@ def tile_attend_gslot_q_kernel(tc, qT, kT, dp, us, ts, wt, offs, out):
             nc.sync.dma_start(out_rows[:, first:end, block(x)], result[:])
 
         g_form(0)
-        g_form(1)
-        g_quantise(0)
-        kt_quantise(1, "neg_eh2")
-        product(0, 0, PACK, "scores0", nc.scalar.copy)
-        g_form(2)
-        g_quantise(1)
-        product(1, 0, PACK, "scores1", nc.scalar.copy)
-        g_form(3)
-        g_quantise(2)
-        product(2, 0, PACK, "scores2", nc.scalar.copy)
+        for x in range(LAST):
+            g_form(x + 1, 0, P // 2)
+            g_quantise(x)
+            product(x, 0, PACK, "scores%d" % x, nc.scalar.copy)
+            g_form(x + 1, P // 2, P)
         g_quantise(3)
         product(3, 0, 2, "scores3", nc.vector.tensor_copy)
         product(3, 2, PACK, "h_ps0", nc.scalar.copy)

@@ -89,7 +89,7 @@ def tile_attend_gslot_q_kernel(tc, qT, kT, dp, us, ts, wt, offs, out):
         wt_col = to_columns("wt_col", [wt_row[:, block(b)] for b in range(PACK)], "h_ps1")
 
         k_words = tile("k_words", [P, PACK, P, PACK], BF16)
-        kt_scales = tiles("kt_scales", 2, [P, 2 * P], U8)
+        kt_scales = tiles("kt_scales", PACK, [P, P], U8)
         kt_codes = {}
 
         def k_gather(j):
@@ -103,16 +103,18 @@ def tile_attend_gslot_q_kernel(tc, qT, kT, dp, us, ts, wt, offs, out):
                 nc.tensor.transpose(turned[:, block(t)], k_words[:, t, :, j], ident16[:])
             return turned[:, 0:R].rearrange("s (t p) -> s p t", t=PACK)
 
-        kt_pair = tile("kt_pair", [P, 2, P, PACK], BF16)
-        for j in range(2):
+        kt_words = tiles("kt_words", LAST, [P, P, PACK], BF16)
+
+        def kt_quantise(j, on):
+            kt_codes[j] = tile("kt_codes%d" % j, [P, P], U32, on)
+            nc.vector.quantize_mx(kt_codes[j][:].bitcast(E4M3), kt_scales[j][:], kt_words[j][:].rearrange("s p t -> s (p t)"))
+
+        for j in range(PACK):
             k_gather(j)
-            nc.scalar.copy(kt_pair[:, j, :, :], kt_turn(j, "scores%d" % j))
-        k_gather(2)
-        kt_codes[0] = tile("kt_codes0", [P, 2 * P], U32, "k_plane2")
-        nc.vector.quantize_mx(kt_codes[0][:].bitcast(E4M3), kt_scales[0][:], kt_pair[:].rearrange("s v p t -> s (v p t)"))
-        kt_third = tile("kt_third", [P, P, PACK], BF16)
-        nc.scalar.copy(kt_third[:], kt_turn(2, "scores2"))
-        k_gather(LAST)
+            if j > 0:
+                kt_quantise(j - 1, "k_plane%d" % j)
+            if j < LAST:
+                nc.scalar.copy(kt_words[j][:], kt_turn(j, "scores%d" % j))
         kt_last_ps = kt_turn(LAST, "kt_last_ps")
         k_codes = tile("k_codes", [P, SLOTS], U32)
         k_scales = tile("k_scales", [P, SLOTS], U8)
@@ -126,17 +128,12 @@ def tile_attend_gslot_q_kernel(tc, qT, kT, dp, us, ts, wt, offs, out):
                 q_words[c][:].rearrange("p (n x) j -> p n j x", x=4),
                 q_raw[c][:].rearrange("p j (n x) -> p n j x", x=4),
             )
-        kt_last = tile("kt_last", [P, P, PACK], BF16, "q_raw0")
-        nc.scalar.copy(kt_last[:], kt_last_ps)
+        kt_words.append(tile("kt_words%d" % LAST, [P, P, PACK], BF16, "q_raw0"))
+        nc.scalar.copy(kt_words[LAST][:], kt_last_ps)
         scores = [bank("scores%d" % t) for t in range(PACK)]
         for c in range(2):
             cols = slice(c * HALF, (c + 1) * HALF)
             nc.vector.quantize_mx(q_codes[:, cols].bitcast(E4M3), q_scales[:, cols], q_words[c][:].rearrange("p r j -> p (r j)"))
-        kt_codes[1] = tile("kt_codes1", [P, 2 * P], U32, "q_words0")
-        for v, words in enumerate((kt_third, kt_last)):
-            nc.vector.quantize_mx(
-                kt_codes[1][:, block(v)].bitcast(E4M3), kt_scales[1][:, block(v)], words[:].rearrange("s p t -> s (p t)")
-            )
 
         def score(target, t, first, end):
             nc.tensor.matmul_mx(
@@ -218,6 +215,7 @@ def tile_attend_gslot_q_kernel(tc, qT, kT, dp, us, ts, wt, offs, out):
         nc.gpsimd.tensor_tensor(h[LAST][:], dp_sb[LAST][:], wt_sb[:], ALU.mult)
 
         logits(0, head, 0, HALF)
+        kt_quantise(LAST, "q_words0")
         logits(0, scores[0], HALF, R)
         logits(1, scores[1], 0, HALF)
         exponentials(0)
@@ -285,24 +283,31 @@ def tile_attend_gslot_q_kernel(tc, qT, kT, dp, us, ts, wt, offs, out):
             g_scales[x] = tile("g_scales%d" % x, [P, P], U8)
             nc.vector.quantize_mx(g_codes[x][:].bitcast(E5M2), g_scales[x][:], g_words[x][:].rearrange("s r t -> s (r t)"))
 
-        def product(x, first, end, on, copy):
+        def passes(x, first, end, on):
             acc = bank("acc%d_%d" % (x, first), on)
             for j in range(first, end):
                 nc.tensor.matmul_mx(
-                    acc[:, block(j - first)], lhsT=kt_codes[j // 2][:, block(j % 2)].bitcast(E4M3),
-                    lhsT_scale=kt_scales[j // 2][:, block(j % 2)],
+                    acc[:, block(j - first)], lhsT=kt_codes[j][:].bitcast(E4M3), lhsT_scale=kt_scales[j][:],
                     rhs=g_codes[x][:].bitcast(E5M2), rhs_scale=g_scales[x][:], start=True, stop=True,
                 )
+            return acc[:, 0:(end - first) * P]
+
+        def product(x, first, end, on, copy):
+            acc = passes(x, first, end, on)
             result = tile("result%d_%d" % (x, first), [P, end - first, P], F32)
-            copy(result[:].rearrange("p j r -> p (j r)"), acc[:, 0:(end - first) * P])
+            copy(result[:].rearrange("p j r -> p (j r)"), acc)
             nc.sync.dma_start(out_rows[:, first:end, block(x)], result[:])
 
         g_form(0)
         for x in range(LAST):
             g_form(x + 1, 0, P // 2)
             g_quantise(x)
-            product(x, 0, PACK, "scores%d" % x, nc.scalar.copy)
+            product(x, 0, 2, ("kt_last_ps", "h_ps0", "h_ps1")[x], nc.scalar.copy)
+            product(x, 2, PACK, "scores%d" % x, nc.scalar.copy)
             g_form(x + 1, P // 2, P)
         g_quantise(3)
-        product(3, 0, 2, "scores3", nc.vector.tensor_copy)
-        product(3, 2, PACK, "h_ps0", nc.scalar.copy)
+        product(LAST, 0, 2, "scores3", nc.scalar.copy)
+        result_last = tile("result_last", [P, 2, P], F32)
+        for v in range(2):
+            nc.vector.tensor_copy(result_last[:, v, :], passes(LAST, 2 + v, 3 + v, ("h_ps2", "kt_last_ps")[v]))
+        nc.sync.dma_start(out_rows[:, 2:PACK, block(LAST)], result_last[:])

@@ -34,39 +34,38 @@ def tile_attend_gslot_q_kernel(tc, qT, kT, dp, us, ts, wt, offs, out):
         def tiles(name, count, shape, dtype):
             return [tile("%s%d" % (name, x), shape, dtype) for x in range(count)]
 
-        def bank(name, on=None):
-            return ps.tile([P, R], F32, name=name, tag=on or name)
+        def bank(name, on):
+            return ps.tile([P, R], F32, name=name, tag=on)
 
         def block(x):
             return slice(x * P, (x + 1) * P)
+
+        def half(c):
+            return slice(c * HALF, (c + 1) * HALF)
 
         def column(stats, x):
             return stats[:, x:x + 1]
 
         offsets = sb.tile([P, SLOTS // 16], U16, name="offsets")
         ts_row = tile("ts_row", [P, TOKENS], F32)
-        wt_row = tile("wt_row", [P, R], F32)
-        nc.vector.memset(ts_row[:], 0.0)
-        nc.vector.memset(wt_row[:], 0.0)
+        uw_row = tile("uw_row", [P, R], F32)
+        nc.vector.memset(uw_row[0:P - 2, :], 0.0)
+        nc.vector.memset(ts_row[0:P - 1, :], 0.0)
         k_plane = tiles("k_plane", PACK, [P, TOKENS], F32)
         k_rows = kT.rearrange("(p j) n -> p j n", j=PACK)
         nc.sync.dma_start(k_plane[0][:], k_rows[:, 0, :])
         nc.sync.dma_start(offsets[:], offs)
-        nc.sync.dma_start(k_plane[1][:], k_rows[:, 1, :])
-        nc.sync.dma_start(ts_row[0:1, :], ts[0:1, :])
-        nc.sync.dma_start(wt_row[0:1, :], wt[0:1, :])
-        for j in range(2, PACK):
+        nc.sync.dma_start(uw_row[P - 2:P - 1, :], us[0:1, :])
+        nc.sync.dma_start(uw_row[P - 1:P, :], wt[0:1, :])
+        nc.sync.dma_start(ts_row[P - 1:P, :], ts[0:1, :])
+        for j in range(1, PACK):
             nc.sync.dma_start(k_plane[j][:], k_rows[:, j, :])
         q_raw = tiles("q_raw", 2, [P, PACK, HALF], F32)
         q_rows = qT.rearrange("(p j) r -> p j r", j=PACK)
-        for c in range(2):
-            nc.sync.dma_start(q_raw[c][:], q_rows[:, :, c * HALF:(c + 1) * HALF])
-        us_sb = tile("us_sb", [P, R], F32)
-        wt_sb = tile("wt_sb", [P, R], F32)
         dp_sb = tiles("dp_sb", PACK, [P, R], F32)
         dp_rows = dp.rearrange("(s t) r -> s t r", t=PACK)
-        nc.sync.dma_start(us_sb[:], us)
-        nc.sync.dma_start(wt_sb[:], wt)
+        for c in range(2):
+            nc.sync.dma_start(q_raw[c][:], q_rows[:, :, half(c)])
         for t in (0, LAST, 1, 2):
             nc.sync.dma_start(dp_sb[t][:], dp_rows[:, t, :])
 
@@ -75,22 +74,36 @@ def tile_attend_gslot_q_kernel(tc, qT, kT, dp, us, ts, wt, offs, out):
         ident16 = tile("ident16", [P, P], BF16)
         make_identity(nc, ident16[:])
 
-        def to_columns(name, blocks, on):
-            turned = bank(name + "_ps", on)
+        def turn(target, blocks):
             for x in range(PACK):
-                nc.tensor.transpose(turned[:, block(x)], blocks[x], ident[:])
-            columns = tile(name, [P, PACK], F32)
-            nc.scalar.activation(columns[:], turned[:, ::P], ACT.Copy)
-            return columns
+                nc.tensor.transpose(target[:, block(x)], blocks[x], ident[:])
+            return target
 
-        ts_listed = tile("ts_listed", [P, SLOTS], F32)
-        nc.vector.tensor_copy(ts_listed[:], ts_row[:].indirect(offsets[:]))
-        ts_col = to_columns("ts_col", [ts_listed[:, t::PACK] for t in range(PACK)], "h_ps0")
-        wt_col = to_columns("wt_col", [wt_row[:, block(b)] for b in range(PACK)], "h_ps1")
+        uw_ps = turn(bank("uw_ps", "h0"), [uw_row[:, block(b)] for b in range(PACK)])
+        uw_col = tile("uw_col", [P, PACK, 2], F32)
+        nc.scalar.activation(uw_col[:], uw_ps[:].rearrange("x (b m) -> x b m", b=PACK)[:, :, P - 2:P], ACT.Copy)
+
+        def spread(name, which, on):
+            turned = turn(bank(name + "_ps", on), [uw_col[:, b, which:which + 1].to_broadcast([P, P]) for b in range(PACK)])
+            whole = tile(name, [P, R], F32)
+            nc.scalar.copy(whole[:], turned[:])
+            return whole
+
+        us_sb = spread("us_sb", 0, "h1")
+        wt_sb = spread("wt_sb", 1, "h2")
+
+        ts_listed = tile("ts_listed", [P, SLOTS], F32, "uw_row")
+        nc.scalar.activation(ts_listed[:], ts_row[:].indirect(offsets[:]), ACT.Copy)
+        ts_ps = turn(bank("ts_ps", "h0"), [ts_listed[:, t::PACK] for t in range(PACK)])
+        ts_col = tile("ts_col", [P, PACK], F32)
+        nc.scalar.copy(ts_col[:], ts_ps[:, P - 1::P])
+        ts_us = tiles("ts_us", PACK, [P, R], F32)
+        for t in range(PACK):
+            nc.scalar.activation(ts_us[t][:], us_sb[:], ACT.Copy, scale=column(ts_col, t))
 
         k_words = tile("k_words", [P, PACK, P, PACK], BF16)
         kt_scales = tiles("kt_scales", PACK, [P, P], U8)
-        kt_codes = {}
+        kt_words, kt_codes = {}, {}
 
         def k_gather(j):
             nc.vector.tensor_copy(
@@ -103,7 +116,9 @@ def tile_attend_gslot_q_kernel(tc, qT, kT, dp, us, ts, wt, offs, out):
                 nc.tensor.transpose(turned[:, block(t)], k_words[:, t, :, j], ident16[:])
             return turned[:, 0:R].rearrange("s (t p) -> s p t", t=PACK)
 
-        kt_words = tiles("kt_words", LAST, [P, P, PACK], BF16)
+        def kt_lay(j, turned, on=None):
+            kt_words[j] = tile("kt_words%d" % j, [P, P, PACK], BF16, on)
+            nc.scalar.copy(kt_words[j][:], turned)
 
         def kt_quantise(j, on):
             kt_codes[j] = tile("kt_codes%d" % j, [P, P], U32, on)
@@ -114,8 +129,8 @@ def tile_attend_gslot_q_kernel(tc, qT, kT, dp, us, ts, wt, offs, out):
             if j > 0:
                 kt_quantise(j - 1, "k_plane%d" % j)
             if j < LAST:
-                nc.scalar.copy(kt_words[j][:], kt_turn(j, "scores%d" % j))
-        kt_last_ps = kt_turn(LAST, "kt_last_ps")
+                kt_lay(j, kt_turn(j, "s%d" % j))
+        kt_last_ps = kt_turn(LAST, "x")
         k_codes = tile("k_codes", [P, SLOTS], U32)
         k_scales = tile("k_scales", [P, SLOTS], U8)
         nc.vector.quantize_mx(k_codes[:].bitcast(E4M3), k_scales[:], k_words[:].rearrange("p t s j -> p (t s j)"))
@@ -128,141 +143,129 @@ def tile_attend_gslot_q_kernel(tc, qT, kT, dp, us, ts, wt, offs, out):
                 q_words[c][:].rearrange("p (n x) j -> p n j x", x=4),
                 q_raw[c][:].rearrange("p j (n x) -> p n j x", x=4),
             )
-        kt_words.append(tile("kt_words%d" % LAST, [P, P, PACK], BF16, "q_raw0"))
-        nc.scalar.copy(kt_words[LAST][:], kt_last_ps)
-        scores = [bank("scores%d" % t) for t in range(PACK)]
-        for c in range(2):
-            cols = slice(c * HALF, (c + 1) * HALF)
-            nc.vector.quantize_mx(q_codes[:, cols].bitcast(E4M3), q_scales[:, cols], q_words[c][:].rearrange("p r j -> p (r j)"))
+        kt_lay(LAST, kt_last_ps, "q_raw0")
 
-        def score(target, t, first, end):
+        def q_quantise(c):
+            nc.vector.quantize_mx(q_codes[:, half(c)].bitcast(E4M3), q_scales[:, half(c)], q_words[c][:].rearrange("p r j -> p (r j)"))
+
+        def score(target, t, cols):
             nc.tensor.matmul_mx(
-                target[:, first:end], lhsT=k_codes[:, block(t)].bitcast(E4M3), lhsT_scale=k_scales[:, block(t)],
-                rhs=q_codes[:, first:end].bitcast(E4M3), rhs_scale=q_scales[:, first:end], start=True, stop=True,
+                target[:, cols], lhsT=k_codes[:, block(t)].bitcast(E4M3), lhsT_scale=k_scales[:, block(t)],
+                rhs=q_codes[:, cols].bitcast(E4M3), rhs_scale=q_scales[:, cols], start=True, stop=True,
             )
-
-        head = bank("scores_head", "h_ps2")
-        score(head, 0, 0, HALF)
-        score(scores[0], 0, HALF, R)
-        dp_ps = {}
-
-        def dp_turn(t):
-            dp_ps[t] = bank("dp_ps%d" % t, "h_ps%d" % t)
-            for b in range(PACK):
-                nc.tensor.transpose(dp_ps[t][:, block(b)], dp_sb[t][:, block(b)], ident[:])
-
-        score(scores[1], 1, 0, R)
-        dp_turn(0)
-        score(scores[2], 2, 0, R)
-        score(scores[3], 3, 0, R)
-        dp_turn(1)
-        dp_turn(2)
 
         z = tiles("z", PACK, [P, R], F32)
         e = tiles("e", PACK, [P, R], F32)
         neg_max = tiles("neg_max", PACK, [P, 1], F32)
         tot = tile("tot", [P, PACK], F32)
         rtot = tile("rtot", [P, PACK], F32)
+        rtot2 = tile("rtot2", [P, LAST], F32)
+        neg_sum = tile("neg_sum", [P, LAST], F32)
+        bias = tile("bias", [P, LAST], F32)
         left = tiles("left", 2, [P, PACK, HALF], F32)
         right = tile("right", [P, PACK, R], F32)
-        h = {}
+        h_turned = {}
+        neg_eh = tiles("neg_eh", LAST, [P, R], F32)
+        h, dp_ps = {}, {}
 
-        def logits(t, source, first, end):
-            nc.vector.scalar_tensor_tensor(
-                z[t][:, first:end], source[:, first:end], column(ts_col, t), us_sb[:, first:end], ALU.mult, ALU.mult
-            )
+        def logits(t, source, cols):
+            nc.vector.tensor_tensor(z[t][:, cols], source[:, cols], ts_us[t][:, cols], ALU.mult)
+
+        def maximum(t):
+            nc.vector.tensor_reduce(neg_max[t][:], z[t][:], AX.X, ALU.max, negate=True)
 
         def exponentials(t):
-            nc.vector.tensor_reduce(neg_max[t][:], z[t][:], AX.X, ALU.max, negate=True)
             nc.scalar.activation(e[t][:], z[t][:], ACT.Exp, bias=neg_max[t][:], accum_out=column(tot, t))
 
         def reciprocals(first, end):
             nc.vector.reciprocal(rtot[:, first:end], tot[:, first:end])
 
-        h_turned = tiles("h_turned", LAST, [P, R], F32)
-        ts_us = tiles("ts_us", PACK, [P, R], F32)
-        neg_eh = tiles("neg_eh", LAST, [P, R], F32)
-        neg_sum = tile("neg_sum", [P, LAST], F32)
-        rtot2 = tile("rtot2", [P, LAST], F32)
-        bias = tile("bias", [P, LAST], F32)
+        def dp_turn(t):
+            dp_ps[t] = turn(bank("dp_ps%d" % t, "h%d" % t), [dp_sb[t][:, block(b)] for b in range(PACK)])
 
-        def h_turn(t):
+        def h_make(t, on=None):
+            h_turned[t] = tile("h_turned%d" % t, [P, R], F32, on)
             for b in range(PACK):
-                nc.scalar.activation(h_turned[t][:, block(b)], dp_ps[t][:, block(b)], ACT.Copy, scale=column(wt_col, b))
+                nc.scalar.activation(h_turned[t][:, block(b)], dp_ps[t][:, block(b)], ACT.Copy, scale=uw_col[:, b, 1:2])
 
-        def h_turn_back(t):
-            h[t] = bank("h_ps%d" % t)
-            for b in range(PACK):
-                nc.tensor.transpose(h[t][:, block(b)], h_turned[t][:, block(b)], ident[:])
+        def h_back(t):
+            h[t] = turn(bank("h_ps%d" % t, "h%d" % t), [h_turned[t][:, block(b)] for b in range(PACK)])
 
-        def squared_reciprocal(t):
-            nc.scalar.activation(column(rtot2, t), column(rtot, t), ACT.Copy, scale=column(rtot, t))
+        def scaled(target, source, factor, t):
+            nc.scalar.activation(column(target, t), column(source, t), ACT.Copy, scale=column(factor, t))
 
         def row_sum(t):
             nc.vector.scalar_tensor_tensor(
                 neg_eh[t][:], e[t][:], -1.0, h[t][:], ALU.mult, ALU.mult, accum_out=column(neg_sum, t)
             )
 
-        def centre(t):
-            nc.scalar.activation(column(bias, t), column(neg_sum, t), ACT.Copy, scale=column(rtot2, t))
-
         def left_on_scalar(t, c):
             nc.scalar.activation(
-                left[c][:, t, :], h[t][:, c * HALF:(c + 1) * HALF], ACT.Identity, bias=column(bias, t), scale=column(rtot, t)
+                left[c][:, t, :], h[t][:, half(c)], ACT.Identity, bias=column(bias, t), scale=column(rtot, t)
             )
 
+        head = bank("head", "h0")
+        scores = [bank("scores%d" % t, on) for t, on in enumerate(("h1", "h2", "s2", "s3"))]
+        q_quantise(0)
+        q_quantise(1)
+        score(head, 0, half(0))
+        score(scores[0], 0, half(1))
+        score(scores[1], 1, slice(0, R))
+        dp_turn(0)
+        score(scores[2], 2, slice(0, R))
+        score(scores[LAST], LAST, slice(0, R))
+        dp_turn(1)
+        dp_turn(2)
         h[LAST] = tile("h_last", [P, R], F32, "q_words1")
         nc.gpsimd.tensor_tensor(h[LAST][:], dp_sb[LAST][:], wt_sb[:], ALU.mult)
-
-        logits(0, head, 0, HALF)
-        kt_quantise(LAST, "q_words0")
-        logits(0, scores[0], HALF, R)
-        logits(1, scores[1], 0, HALF)
+        logits(0, head, half(0))
+        logits(0, scores[0], half(1))
+        logits(1, scores[1], half(0))
+        maximum(0)
         exponentials(0)
-        h_turn(0)
-        logits(1, scores[1], HALF, R)
-        h_turn_back(0)
+        h_make(0)
+        logits(1, scores[1], half(1))
+        h_back(0)
         for t in range(1, LAST):
-            logits(t + 1, scores[t + 1], 0, R)
+            logits(t + 1, scores[t + 1], slice(0, R))
+            maximum(t)
             exponentials(t)
-            h_turn(t)
-            h_turn_back(t)
+            h_make(t)
+            h_back(t)
+        maximum(LAST)
         exponentials(LAST)
-        for t in range(PACK):
-            nc.scalar.activation(ts_us[t][:], us_sb[:], ACT.Copy, scale=column(ts_col, t))
         for t in range(LAST):
             nc.gpsimd.tensor_tensor(right[:, t, :], e[t][:], ts_us[t][:], ALU.mult)
 
         reciprocals(0, 2)
-        squared_reciprocal(0)
-        squared_reciprocal(1)
+        for t in range(2):
+            scaled(rtot2, rtot, rtot, t)
         row_sum(0)
-        centre(0)
+        scaled(bias, neg_sum, rtot2, 0)
         left_on_scalar(0, 0)
-        left_on_scalar(0, 1)
         row_sum(1)
         reciprocals(2, PACK)
-        squared_reciprocal(2)
-        centre(1)
+        scaled(rtot2, rtot, rtot, 2)
+        scaled(bias, neg_sum, rtot2, 1)
         left_on_scalar(1, 0)
         row_sum(2)
-        centre(2)
+        nc.scalar.activation(right[:, LAST, half(0)], ts_us[LAST][:, half(0)], ACT.Copy, scale=column(rtot, LAST))
+        scaled(bias, neg_sum, rtot2, 2)
         left_on_scalar(2, 0)
-        left_on_scalar(1, 1)
-        left_on_scalar(2, 1)
 
         ph = tile("ph", [P, R], F32)
         mean = tile("mean", [P, 1], F32)
         nc.vector.scalar_tensor_tensor(
             ph[:], e[LAST][:], column(rtot, LAST), h[LAST][:], ALU.mult, ALU.mult, accum_out=mean[:]
         )
-        nc.vector.tensor_scalar(right[:, LAST, :], ts_us[LAST][:], column(rtot, LAST), None, ALU.mult)
+        kt_quantise(LAST, "neg_eh2")
         for c in range(2):
-            cols = slice(c * HALF, (c + 1) * HALF)
             nc.vector.scalar_tensor_tensor(
-                left[c][:, LAST, :], h[LAST][:, cols], mean[:], e[LAST][:, cols], ALU.subtract, ALU.mult
+                left[c][:, LAST, :], h[LAST][:, half(c)], mean[:], e[LAST][:, half(c)], ALU.subtract, ALU.mult
             )
-
+        for t in range(LAST):
+            left_on_scalar(t, 1)
+        nc.scalar.activation(right[:, LAST, half(1)], ts_us[LAST][:, half(1)], ACT.Copy, scale=column(rtot, LAST))
 
         out_rows = out.rearrange("(p j) r -> p j r", j=PACK)
         g_words, g_codes, g_scales = {}, {}, {}
@@ -302,12 +305,12 @@ def tile_attend_gslot_q_kernel(tc, qT, kT, dp, us, ts, wt, offs, out):
         for x in range(LAST):
             g_form(x + 1, 0, P // 2)
             g_quantise(x)
-            product(x, 0, 2, ("kt_last_ps", "h_ps0", "h_ps1")[x], nc.scalar.copy)
-            product(x, 2, PACK, "scores%d" % x, nc.scalar.copy)
+            product(x, 0, 2, ("x", "s3", "x")[x], nc.scalar.copy)
+            product(x, 2, PACK, "s%d" % x, nc.scalar.copy)
             g_form(x + 1, P // 2, P)
         g_quantise(3)
-        product(LAST, 0, 2, "scores3", nc.scalar.copy)
+        product(LAST, 0, 2, "h0", nc.scalar.copy)
         result_last = tile("result_last", [P, 2, P], F32)
         for v in range(2):
-            nc.vector.tensor_copy(result_last[:, v, :], passes(LAST, 2 + v, 3 + v, ("h_ps2", "kt_last_ps")[v]))
+            nc.vector.tensor_copy(result_last[:, v, :], passes(LAST, 2 + v, 3 + v, ("h1", "h2")[v]))
         nc.sync.dma_start(out_rows[:, 2:PACK, block(LAST)], result_last[:])

@@ -140,8 +140,8 @@ def tile_attend_gslot_q_kernel(tc, qT, kT, dp, us, ts, wt, offs, out):
         q_scales = tile("q_scales", [P, R], U8)
         for c, copy in enumerate((nc.scalar.copy, nc.vector.tensor_copy)):
             copy(
-                q_words[c][:].rearrange("p (n x) j -> p n j x", x=4),
-                q_raw[c][:].rearrange("p j (n x) -> p n j x", x=4),
+                q_words[c][:].rearrange("p (n x) j -> p n j x", x=2),
+                q_raw[c][:].rearrange("p j (n x) -> p n j x", x=2),
             )
         kt_lay(LAST, kt_last_ps, "q_raw0")
 

@@ -66,7 +66,7 @@ def tile_attend_gslot_q_kernel(tc, qT, kT, dp, us, ts, wt, offs, out):
         dp_rows = dp.rearrange("(s t) r -> s t r", t=PACK)
         for c in range(2):
             nc.sync.dma_start(q_raw[c][:], q_rows[:, :, half(c)])
-        for t in (0, LAST, 1, 2):
+        for t in (LAST, 0, 2, 1):
             nc.sync.dma_start(dp_sb[t][:], dp_rows[:, t, :])
 
         ident = tile("ident", [P, P], F32)
@@ -100,6 +100,8 @@ def tile_attend_gslot_q_kernel(tc, qT, kT, dp, us, ts, wt, offs, out):
         ts_us = tiles("ts_us", PACK, [P, R], F32)
         for t in range(PACK):
             nc.scalar.activation(ts_us[t][:], us_sb[:], ACT.Copy, scale=column(ts_col, t))
+        ts_us_half = tile("ts_us_half", [P, HALF], F32)
+        nc.scalar.activation(ts_us_half[:], us_sb[:, half(0)], ACT.Copy, scale=column(ts_col, 2))
 
         k_words = tile("k_words", [P, PACK, P, PACK], BF16)
         kt_scales = tiles("kt_scales", PACK, [P, P], U8)
@@ -165,7 +167,7 @@ def tile_attend_gslot_q_kernel(tc, qT, kT, dp, us, ts, wt, offs, out):
         left = tiles("left", 2, [P, PACK, HALF], F32)
         right = tile("right", [P, PACK, R], F32)
         h_turned = {}
-        neg_eh = tiles("neg_eh", LAST, [P, R], F32)
+        neg_eh = {}
         h, dp_ps = {}, {}
 
         def logits(t, source, cols):
@@ -189,12 +191,13 @@ def tile_attend_gslot_q_kernel(tc, qT, kT, dp, us, ts, wt, offs, out):
                 nc.scalar.activation(h_turned[t][:, block(b)], dp_ps[t][:, block(b)], ACT.Copy, scale=uw_col[:, b, 1:2])
 
         def h_back(t):
-            h[t] = turn(bank("h_ps%d" % t, "h%d" % t), [h_turned[t][:, block(b)] for b in range(PACK)])
+            h[t] = turn(bank("h_ps%d" % t, "s%d" % t), [h_turned[t][:, block(b)] for b in range(PACK)])
 
         def scaled(target, source, factor, t):
             nc.scalar.activation(column(target, t), column(source, t), ACT.Copy, scale=column(factor, t))
 
-        def row_sum(t):
+        def row_sum(t, on=None):
+            neg_eh[t] = tile("neg_eh%d" % t, [P, R], F32, on)
             nc.vector.scalar_tensor_tensor(
                 neg_eh[t][:], e[t][:], -1.0, h[t][:], ALU.mult, ALU.mult, accum_out=column(neg_sum, t)
             )
@@ -215,27 +218,28 @@ def tile_attend_gslot_q_kernel(tc, qT, kT, dp, us, ts, wt, offs, out):
         score(scores[2], 2, slice(0, R))
         score(scores[LAST], LAST, slice(0, R))
         dp_turn(1)
-        dp_turn(2)
         h[LAST] = tile("h_last", [P, R], F32, "q_words1")
         nc.gpsimd.tensor_tensor(h[LAST][:], dp_sb[LAST][:], wt_sb[:], ALU.mult)
+        h[2] = tile("h_third", [P, R], F32, "dp_sb3")
+        nc.gpsimd.tensor_tensor(h[2][:], dp_sb[2][:], wt_sb[:], ALU.mult)
         logits(0, head, half(0))
         logits(0, scores[0], half(1))
-        logits(1, scores[1], half(0))
-        maximum(0)
-        exponentials(0)
-        h_make(0)
-        logits(1, scores[1], half(1))
-        h_back(0)
-        for t in range(1, LAST):
-            logits(t + 1, scores[t + 1], slice(0, R))
+        logits(1, scores[1], slice(0, R))
+        for t in range(2):
             maximum(t)
             exponentials(t)
-            h_make(t)
-            h_back(t)
-        maximum(LAST)
-        exponentials(LAST)
-        for t in range(LAST):
+        h_make(0, "z1")
+        h_back(0)
+        h_make(1)
+        h_back(1)
+        for t in range(2, PACK):
+            logits(t, scores[t], slice(0, R))
+        for t in range(2, PACK):
+            maximum(t)
+            exponentials(t)
+        for t in range(2):
             nc.gpsimd.tensor_tensor(right[:, t, :], e[t][:], ts_us[t][:], ALU.mult)
+        nc.gpsimd.tensor_tensor(right[:, 2, half(0)], e[2][:, half(0)], ts_us_half[:], ALU.mult)
 
         reciprocals(0, 2)
         for t in range(2):
@@ -248,8 +252,8 @@ def tile_attend_gslot_q_kernel(tc, qT, kT, dp, us, ts, wt, offs, out):
         scaled(rtot2, rtot, rtot, 2)
         scaled(bias, neg_sum, rtot2, 1)
         left_on_scalar(1, 0)
-        row_sum(2)
         nc.scalar.activation(right[:, LAST, half(0)], ts_us[LAST][:, half(0)], ACT.Copy, scale=column(rtot, LAST))
+        row_sum(2, "ts_us_half")
         scaled(bias, neg_sum, rtot2, 2)
         left_on_scalar(2, 0)
 
@@ -258,13 +262,19 @@ def tile_attend_gslot_q_kernel(tc, qT, kT, dp, us, ts, wt, offs, out):
         nc.vector.scalar_tensor_tensor(
             ph[:], e[LAST][:], column(rtot, LAST), h[LAST][:], ALU.mult, ALU.mult, accum_out=mean[:]
         )
-        kt_quantise(LAST, "neg_eh2")
+        nc.vector.scalar_tensor_tensor(
+            right[:, 2, half(1)], e[2][:, half(1)], column(rtot, 2), ts_us[2][:, half(1)], ALU.mult, ALU.mult
+        )
         for c in range(2):
             nc.vector.scalar_tensor_tensor(
                 left[c][:, LAST, :], h[LAST][:, half(c)], mean[:], e[LAST][:, half(c)], ALU.subtract, ALU.mult
             )
-        for t in range(LAST):
+        kt_quantise(LAST, "ph")
+        neg_mean = tile("neg_mean", [P, PACK], F32)
+        scaled(neg_mean, neg_sum, rtot, 2)
+        for t in range(2):
             left_on_scalar(t, 1)
+        nc.scalar.activation(left[1][:, 2, :], h[2][:, half(1)], ACT.Identity, bias=column(neg_mean, 2))
         nc.scalar.activation(right[:, LAST, half(1)], ts_us[LAST][:, half(1)], ACT.Copy, scale=column(rtot, LAST))
 
         out_rows = out.rearrange("(p j) r -> p j r", j=PACK)
@@ -305,12 +315,12 @@ def tile_attend_gslot_q_kernel(tc, qT, kT, dp, us, ts, wt, offs, out):
         for x in range(LAST):
             g_form(x + 1, 0, P // 2)
             g_quantise(x)
-            product(x, 0, 2, ("x", "s3", "x")[x], nc.scalar.copy)
-            product(x, 2, PACK, "s%d" % x, nc.scalar.copy)
+            product(x, 0, 2, ("x", "h1", "s2")[x], nc.scalar.copy)
+            product(x, 2, PACK, ("h0", "h2", "s3")[x], nc.scalar.copy)
             g_form(x + 1, P // 2, P)
         g_quantise(3)
-        product(LAST, 0, 2, "h0", nc.scalar.copy)
+        product(LAST, 0, 2, "x", nc.scalar.copy)
         result_last = tile("result_last", [P, 2, P], F32)
         for v in range(2):
-            nc.vector.tensor_copy(result_last[:, v, :], passes(LAST, 2 + v, 3 + v, ("h1", "h2")[v]))
+            nc.vector.tensor_copy(result_last[:, v, :], passes(LAST, 2 + v, 3 + v, ("s0", "s1")[v]))
         nc.sync.dma_start(out_rows[:, 2:PACK, block(LAST)], result_last[:])

@@ -100,8 +100,8 @@ def tile_attend_gslot_q_kernel(tc, qT, kT, dp, us, ts, wt, offs, out):
         ts_us = tiles("ts_us", PACK, [P, R], F32)
         for t in range(PACK):
             nc.scalar.activation(ts_us[t][:], us_sb[:], ACT.Copy, scale=column(ts_col, t))
-        ts_us_half = tile("ts_us_half", [P, HALF], F32)
-        nc.scalar.activation(ts_us_half[:], us_sb[:, half(0)], ACT.Copy, scale=column(ts_col, 2))
+        ts_us_half = tile("ts_us_half", [P, P], F32)
+        nc.scalar.activation(ts_us_half[:], us_sb[:, block(0)], ACT.Copy, scale=column(ts_col, 2))
 
         k_words = tile("k_words", [P, PACK, P, PACK], BF16)
         kt_scales = tiles("kt_scales", PACK, [P, P], U8)
@@ -239,7 +239,7 @@ def tile_attend_gslot_q_kernel(tc, qT, kT, dp, us, ts, wt, offs, out):
             exponentials(t)
         for t in range(2):
             nc.gpsimd.tensor_tensor(right[:, t, :], e[t][:], ts_us[t][:], ALU.mult)
-        nc.gpsimd.tensor_tensor(right[:, 2, half(0)], e[2][:, half(0)], ts_us_half[:], ALU.mult)
+        nc.gpsimd.tensor_tensor(right[:, 2, block(0)], e[2][:, block(0)], ts_us_half[:], ALU.mult)
 
         reciprocals(0, 2)
         for t in range(2):
@@ -255,7 +255,10 @@ def tile_attend_gslot_q_kernel(tc, qT, kT, dp, us, ts, wt, offs, out):
         nc.scalar.activation(right[:, LAST, half(0)], ts_us[LAST][:, half(0)], ACT.Copy, scale=column(rtot, LAST))
         row_sum(2, "ts_us_half")
         scaled(bias, neg_sum, rtot2, 2)
-        left_on_scalar(2, 0)
+        nc.scalar.activation(left[0][:, 2, block(0)], h[2][:, block(0)], ACT.Identity, bias=column(bias, 2), scale=column(rtot, 2))
+        neg_mean = tile("neg_mean", [P, PACK], F32)
+        scaled(neg_mean, neg_sum, rtot, 2)
+        nc.scalar.activation(left[0][:, 2, block(1)], h[2][:, block(1)], ACT.Identity, bias=column(neg_mean, 2))
 
         ph = tile("ph", [P, R], F32)
         mean = tile("mean", [P, 1], F32)
@@ -263,15 +266,13 @@ def tile_attend_gslot_q_kernel(tc, qT, kT, dp, us, ts, wt, offs, out):
             ph[:], e[LAST][:], column(rtot, LAST), h[LAST][:], ALU.mult, ALU.mult, accum_out=mean[:]
         )
         nc.vector.scalar_tensor_tensor(
-            right[:, 2, half(1)], e[2][:, half(1)], column(rtot, 2), ts_us[2][:, half(1)], ALU.mult, ALU.mult
+            right[:, 2, P:R], e[2][:, P:R], column(rtot, 2), ts_us[2][:, P:R], ALU.mult, ALU.mult
         )
         for c in range(2):
             nc.vector.scalar_tensor_tensor(
                 left[c][:, LAST, :], h[LAST][:, half(c)], mean[:], e[LAST][:, half(c)], ALU.subtract, ALU.mult
             )
         kt_quantise(LAST, "ph")
-        neg_mean = tile("neg_mean", [P, PACK], F32)
-        scaled(neg_mean, neg_sum, rtot, 2)
         for t in range(2):
             left_on_scalar(t, 1)
         nc.scalar.activation(left[1][:, 2, :], h[2][:, half(1)], ACT.Identity, bias=column(neg_mean, 2))

@@ -211,6 +211,7 @@ def tile_attend_gslot_q_kernel(tc, qT, kT, dp, us, ts, wt, offs, out):
         scores = [bank("scores%d" % t, on) for t, on in enumerate(("h1", "h2", "s2", "s3"))]
         q_quantise(0)
         q_quantise(1)
+        kt_quantise(LAST, "q_words0")
         score(head, 0, half(0))
         score(scores[0], 0, half(1))
         score(scores[1], 1, slice(0, R))
@@ -218,7 +219,7 @@ def tile_attend_gslot_q_kernel(tc, qT, kT, dp, us, ts, wt, offs, out):
         score(scores[2], 2, slice(0, R))
         score(scores[LAST], LAST, slice(0, R))
         dp_turn(1)
-        h[LAST] = tile("h_last", [P, R], F32, "q_words1")
+        h[LAST] = tile("h_last", [P, R], F32, "q_raw0")
         nc.gpsimd.tensor_tensor(h[LAST][:], dp_sb[LAST][:], wt_sb[:], ALU.mult)
         h[2] = tile("h_third", [P, R], F32, "dp_sb3")
         nc.gpsimd.tensor_tensor(h[2][:], dp_sb[2][:], wt_sb[:], ALU.mult)
@@ -272,7 +273,6 @@ def tile_attend_gslot_q_kernel(tc, qT, kT, dp, us, ts, wt, offs, out):
             nc.vector.scalar_tensor_tensor(
                 left[c][:, LAST, :], h[LAST][:, half(c)], mean[:], e[LAST][:, half(c)], ALU.subtract, ALU.mult
             )
-        kt_quantise(LAST, "ph")
         for t in range(2):
             left_on_scalar(t, 1)
         nc.scalar.activation(left[1][:, 2, :], h[2][:, half(1)], ACT.Identity, bias=column(neg_mean, 2))

@@ -100,8 +100,6 @@ def tile_attend_gslot_q_kernel(tc, qT, kT, dp, us, ts, wt, offs, out):
         ts_us = tiles("ts_us", PACK, [P, R], F32)
         for t in range(PACK):
             nc.scalar.activation(ts_us[t][:], us_sb[:], ACT.Copy, scale=column(ts_col, t))
-        ts_us_half = tile("ts_us_half", [P, P], F32)
-        nc.scalar.activation(ts_us_half[:], us_sb[:, block(0)], ACT.Copy, scale=column(ts_col, 2))
 
         k_words = tile("k_words", [P, PACK, P, PACK], BF16)
         kt_scales = tiles("kt_scales", PACK, [P, P], U8)
@@ -226,10 +224,10 @@ def tile_attend_gslot_q_kernel(tc, qT, kT, dp, us, ts, wt, offs, out):
         logits(0, head, half(0))
         logits(0, scores[0], half(1))
         logits(1, scores[1], slice(0, R))
+        h_make(0)
         for t in range(2):
             maximum(t)
             exponentials(t)
-        h_make(0, "z1")
         h_back(0)
         h_make(1)
         h_back(1)
@@ -240,7 +238,6 @@ def tile_attend_gslot_q_kernel(tc, qT, kT, dp, us, ts, wt, offs, out):
             exponentials(t)
         for t in range(2):
             nc.gpsimd.tensor_tensor(right[:, t, :], e[t][:], ts_us[t][:], ALU.mult)
-        nc.gpsimd.tensor_tensor(right[:, 2, block(0)], e[2][:, block(0)], ts_us_half[:], ALU.mult)
 
         reciprocals(0, 2)
         for t in range(2):
@@ -249,17 +246,15 @@ def tile_attend_gslot_q_kernel(tc, qT, kT, dp, us, ts, wt, offs, out):
         scaled(bias, neg_sum, rtot2, 0)
         left_on_scalar(0, 0)
         row_sum(1)
-        reciprocals(2, PACK)
-        scaled(rtot2, rtot, rtot, 2)
         scaled(bias, neg_sum, rtot2, 1)
         left_on_scalar(1, 0)
+        reciprocals(2, LAST)
+        reciprocals(LAST, PACK)
+        row_sum(2, "ts_us1")
         nc.scalar.activation(right[:, LAST, half(0)], ts_us[LAST][:, half(0)], ACT.Copy, scale=column(rtot, LAST))
-        row_sum(2, "ts_us_half")
-        scaled(bias, neg_sum, rtot2, 2)
-        nc.scalar.activation(left[0][:, 2, block(0)], h[2][:, block(0)], ACT.Identity, bias=column(bias, 2), scale=column(rtot, 2))
         neg_mean = tile("neg_mean", [P, PACK], F32)
         scaled(neg_mean, neg_sum, rtot, 2)
-        nc.scalar.activation(left[0][:, 2, block(1)], h[2][:, block(1)], ACT.Identity, bias=column(neg_mean, 2))
+        nc.scalar.activation(left[0][:, 2, :], h[2][:, half(0)], ACT.Identity, bias=column(neg_mean, 2))
 
         ph = tile("ph", [P, R], F32)
         mean = tile("mean", [P, 1], F32)
@@ -267,7 +262,7 @@ def tile_attend_gslot_q_kernel(tc, qT, kT, dp, us, ts, wt, offs, out):
             ph[:], e[LAST][:], column(rtot, LAST), h[LAST][:], ALU.mult, ALU.mult, accum_out=mean[:]
         )
         nc.vector.scalar_tensor_tensor(
-            right[:, 2, P:R], e[2][:, P:R], column(rtot, 2), ts_us[2][:, P:R], ALU.mult, ALU.mult
+            right[:, 2, :], e[2][:], column(rtot, 2), ts_us[2][:], ALU.mult, ALU.mult
         )
         for c in range(2):
             nc.vector.scalar_tensor_tensor(

@@ -258,12 +258,17 @@ def tile_attend_gslot_q_kernel(tc, qT, kT, dp, us, ts, wt, offs, out):
 
         ph = tile("ph", [P, R], F32)
         mean = tile("mean", [P, 1], F32)
+
+        def right_third(c):
+            nc.vector.scalar_tensor_tensor(
+                right[:, 2, half(c)], e[2][:, half(c)], column(rtot, 2), ts_us[2][:, half(c)], ALU.mult, ALU.mult
+            )
+
+        right_third(0)
         nc.vector.scalar_tensor_tensor(
             ph[:], e[LAST][:], column(rtot, LAST), h[LAST][:], ALU.mult, ALU.mult, accum_out=mean[:]
         )
-        nc.vector.scalar_tensor_tensor(
-            right[:, 2, :], e[2][:], column(rtot, 2), ts_us[2][:], ALU.mult, ALU.mult
-        )
+        right_third(1)
         for c in range(2):
             nc.vector.scalar_tensor_tensor(
                 left[c][:, LAST, :], h[LAST][:, half(c)], mean[:], e[LAST][:, half(c)], ALU.subtract, ALU.mult
@@ -287,10 +292,14 @@ def tile_attend_gslot_q_kernel(tc, qT, kT, dp, us, ts, wt, offs, out):
                 ALU.mult,
             )
 
-        def g_quantise(x):
-            g_codes[x] = tile("g_codes%d" % x, [P, P], U32)
-            g_scales[x] = tile("g_scales%d" % x, [P, P], U8)
-            nc.vector.quantize_mx(g_codes[x][:].bitcast(E5M2), g_scales[x][:], g_words[x][:].rearrange("s r t -> s (r t)"))
+        def g_quantise(x, start=0, stop=P):
+            if start == 0:
+                g_codes[x] = tile("g_codes%d" % x, [P, P], U32)
+                g_scales[x] = tile("g_scales%d" % x, [P, P], U8)
+            nc.vector.quantize_mx(
+                g_codes[x][:, start:stop].bitcast(E5M2), g_scales[x][:, start:stop],
+                g_words[x][:, start:stop, :].rearrange("s r t -> s (r t)"),
+            )
 
         def passes(x, first, end, on):
             acc = bank("acc%d_%d" % (x, first), on)
@@ -301,20 +310,27 @@ def tile_attend_gslot_q_kernel(tc, qT, kT, dp, us, ts, wt, offs, out):
                 )
             return acc[:, 0:(end - first) * P]
 
-        def product(x, first, end, on, copy):
-            acc = passes(x, first, end, on)
+        def leave(x, first, end, acc, copy):
             result = tile("result%d_%d" % (x, first), [P, end - first, P], F32)
             copy(result[:].rearrange("p j r -> p (j r)"), acc)
             nc.sync.dma_start(out_rows[:, first:end, block(x)], result[:])
+
+        def product(x, first, end, on, copy):
+            leave(x, first, end, passes(x, first, end, on), copy)
 
         g_form(0)
         for x in range(LAST):
             g_form(x + 1, 0, P // 2)
             g_quantise(x)
             product(x, 0, 2, ("x", "h1", "s2")[x], nc.scalar.copy)
-            product(x, 2, PACK, ("h0", "h2", "s3")[x], nc.scalar.copy)
+            if x < 2:
+                product(x, 2, PACK, ("h0", "h2")[x], nc.scalar.copy)
+            else:
+                waiting = passes(x, 2, PACK, "s3")
             g_form(x + 1, P // 2, P)
-        g_quantise(3)
+        g_quantise(LAST, 0, P // 2)
+        g_quantise(LAST, P // 2, P)
+        leave(2, 2, PACK, waiting, nc.vector.tensor_copy)
         product(LAST, 0, 2, "x", nc.scalar.copy)
         result_last = tile("result_last", [P, 2, P], F32)
         for v in range(2):

@@ -205,14 +205,15 @@ def tile_attend_gslot_q_kernel(tc, qT, kT, dp, us, ts, wt, offs, out):
                 left[c][:, t, :], h[t][:, half(c)], ACT.Identity, bias=column(bias, t), scale=column(rtot, t)
             )
 
-        head = bank("head", "h0")
+        heads = [bank("head%d" % t, on) for t, on in enumerate(("h0", "s0"))]
         scores = [bank("scores%d" % t, on) for t, on in enumerate(("h1", "h2", "s2", "s3"))]
         q_quantise(0)
         q_quantise(1)
         kt_quantise(LAST, "q_words0")
-        score(head, 0, half(0))
-        score(scores[0], 0, half(1))
-        score(scores[1], 1, slice(0, R))
+        for t in range(2):
+            score(heads[t], t, half(0))
+        for t in range(2):
+            score(scores[t], t, half(1))
         dp_turn(0)
         score(scores[2], 2, slice(0, R))
         score(scores[LAST], LAST, slice(0, R))
@@ -221,9 +222,10 @@ def tile_attend_gslot_q_kernel(tc, qT, kT, dp, us, ts, wt, offs, out):
         nc.gpsimd.tensor_tensor(h[LAST][:], dp_sb[LAST][:], wt_sb[:], ALU.mult)
         h[2] = tile("h_third", [P, R], F32, "dp_sb3")
         nc.gpsimd.tensor_tensor(h[2][:], dp_sb[2][:], wt_sb[:], ALU.mult)
-        logits(0, head, half(0))
-        logits(0, scores[0], half(1))
-        logits(1, scores[1], slice(0, R))
+        for t in range(2):
+            logits(t, heads[t], half(0))
+        for t in range(2):
+            logits(t, scores[t], half(1))
         h_make(0)
         for t in range(2):
             maximum(t)
@@ -310,27 +312,21 @@ def tile_attend_gslot_q_kernel(tc, qT, kT, dp, us, ts, wt, offs, out):
                 )
             return acc[:, 0:(end - first) * P]
 
-        def leave(x, first, end, acc, copy):
+        def product(x, first, end, on, copy):
+            acc = passes(x, first, end, on)
             result = tile("result%d_%d" % (x, first), [P, end - first, P], F32)
             copy(result[:].rearrange("p j r -> p (j r)"), acc)
             nc.sync.dma_start(out_rows[:, first:end, block(x)], result[:])
-
-        def product(x, first, end, on, copy):
-            leave(x, first, end, passes(x, first, end, on), copy)
 
         g_form(0)
         for x in range(LAST):
             g_form(x + 1, 0, P // 2)
             g_quantise(x)
             product(x, 0, 2, ("x", "h1", "s2")[x], nc.scalar.copy)
-            if x < 2:
-                product(x, 2, PACK, ("h0", "h2")[x], nc.scalar.copy)
-            else:
-                waiting = passes(x, 2, PACK, "s3")
+            product(x, 2, PACK, ("h0", "h2", "s3")[x], nc.scalar.copy)
             g_form(x + 1, P // 2, P)
         g_quantise(LAST, 0, P // 2)
         g_quantise(LAST, P // 2, P)
-        leave(2, 2, PACK, waiting, nc.vector.tensor_copy)
         product(LAST, 0, 2, "x", nc.scalar.copy)
         result_last = tile("result_last", [P, 2, P], F32)
         for v in range(2):

@@ -62,11 +62,15 @@ def tile_attend_gslot_q_kernel(tc, qT, kT, dp, us, ts, wt, offs, out):
             nc.sync.dma_start(k_plane[j][:], k_rows[:, j, :])
         q_raw = tiles("q_raw", 2, [P, PACK, HALF], F32)
         q_rows = qT.rearrange("(p j) r -> p j r", j=PACK)
-        dp_sb = tiles("dp_sb", PACK, [P, R], F32)
+        dp_sb = {t: tile("dp_sb%d" % t, [P, R], F32) for t in range(1, PACK)}
         dp_rows = dp.rearrange("(s t) r -> s t r", t=PACK)
         for c in range(2):
             nc.sync.dma_start(q_raw[c][:], q_rows[:, :, half(c)])
-        for t in (LAST, 0, 2, 1):
+        dp_first = tiles("dp_first", 2, [P, HALF], F32)
+        nc.sync.dma_start(dp_first[0][:], dp_rows[:, 0, half(0)])
+        nc.sync.dma_start(dp_sb[LAST][:], dp_rows[:, LAST, :])
+        nc.sync.dma_start(dp_first[1][:], dp_rows[:, 0, half(1)])
+        for t in (2, 1):
             nc.sync.dma_start(dp_sb[t][:], dp_rows[:, t, :])
 
         ident = tile("ident", [P, P], F32)
@@ -164,7 +168,7 @@ def tile_attend_gslot_q_kernel(tc, qT, kT, dp, us, ts, wt, offs, out):
         bias = tile("bias", [P, LAST], F32)
         left = tiles("left", 2, [P, PACK, HALF], F32)
         right = tile("right", [P, PACK, R], F32)
-        h_turned = {}
+        h_turned = tiles("h_turned", 2, [P, R], F32)
         neg_eh = {}
         h, dp_ps = {}, {}
 
@@ -180,13 +184,15 @@ def tile_attend_gslot_q_kernel(tc, qT, kT, dp, us, ts, wt, offs, out):
         def reciprocals(first, end):
             nc.vector.reciprocal(rtot[:, first:end], tot[:, first:end])
 
-        def dp_turn(t):
-            dp_ps[t] = turn(bank("dp_ps%d" % t, "h%d" % t), [dp_sb[t][:, block(b)] for b in range(PACK)])
+        def dp_turn(t, c, source, on):
+            dp_ps[t, c] = bank("dp_ps%d_%d" % (t, c), on)
+            for v in range(2):
+                nc.tensor.transpose(dp_ps[t, c][:, block(v)], source[:, block(v)], ident[:])
 
-        def h_make(t, on=None):
-            h_turned[t] = tile("h_turned%d" % t, [P, R], F32, on)
-            for b in range(PACK):
-                nc.scalar.activation(h_turned[t][:, block(b)], dp_ps[t][:, block(b)], ACT.Copy, scale=uw_col[:, b, 1:2])
+        def h_make(t, c):
+            for v in range(2):
+                b = 2 * c + v
+                nc.scalar.activation(h_turned[t][:, block(b)], dp_ps[t, c][:, block(v)], ACT.Copy, scale=uw_col[:, b, 1:2])
 
         def h_back(t):
             h[t] = turn(bank("h_ps%d" % t, "s%d" % t), [h_turned[t][:, block(b)] for b in range(PACK)])
@@ -205,6 +211,8 @@ def tile_attend_gslot_q_kernel(tc, qT, kT, dp, us, ts, wt, offs, out):
                 left[c][:, t, :], h[t][:, half(c)], ACT.Identity, bias=column(bias, t), scale=column(rtot, t)
             )
 
+        dp_turn(0, 0, dp_first[0], "s1")
+        h_make(0, 0)
         heads = [bank("head%d" % t, on) for t, on in enumerate(("h0", "s0"))]
         scores = [bank("scores%d" % t, on) for t, on in enumerate(("h1", "h2", "s2", "s3"))]
         q_quantise(0)
@@ -214,10 +222,11 @@ def tile_attend_gslot_q_kernel(tc, qT, kT, dp, us, ts, wt, offs, out):
             score(heads[t], t, half(0))
         for t in range(2):
             score(scores[t], t, half(1))
-        dp_turn(0)
+        dp_turn(0, 1, dp_first[1], "h0")
         score(scores[2], 2, slice(0, R))
         score(scores[LAST], LAST, slice(0, R))
-        dp_turn(1)
+        for c, on in enumerate(("h1", "h2")):
+            dp_turn(1, c, dp_sb[1][:, half(c)], on)
         h[LAST] = tile("h_last", [P, R], F32, "q_raw0")
         nc.gpsimd.tensor_tensor(h[LAST][:], dp_sb[LAST][:], wt_sb[:], ALU.mult)
         h[2] = tile("h_third", [P, R], F32, "dp_sb3")
@@ -226,12 +235,13 @@ def tile_attend_gslot_q_kernel(tc, qT, kT, dp, us, ts, wt, offs, out):
             logits(t, heads[t], half(0))
         for t in range(2):
             logits(t, scores[t], half(1))
-        h_make(0)
+        h_make(0, 1)
         for t in range(2):
             maximum(t)
             exponentials(t)
         h_back(0)
-        h_make(1)
+        for c in range(2):
+            h_make(1, c)
         h_back(1)
         for t in range(2, PACK):
             logits(t, scores[t], slice(0, R))

@@ -168,7 +168,7 @@ def tile_attend_gslot_q_kernel(tc, qT, kT, dp, us, ts, wt, offs, out):
         bias = tile("bias", [P, LAST], F32)
         left = tiles("left", 2, [P, PACK, HALF], F32)
         right = tile("right", [P, PACK, R], F32)
-        h_turned = tiles("h_turned", 2, [P, R], F32)
+        h_turned = {}
         neg_eh = {}
         h, dp_ps = {}, {}
 
@@ -189,13 +189,14 @@ def tile_attend_gslot_q_kernel(tc, qT, kT, dp, us, ts, wt, offs, out):
             for v in range(2):
                 nc.tensor.transpose(dp_ps[t, c][:, block(v)], source[:, block(v)], ident[:])
 
-        def h_make(t, c):
+        def h_make(t, c, on=None):
+            h_turned[t, c] = tile("h_turned%d_%d" % (t, c), [P, HALF], F32, on)
             for v in range(2):
                 b = 2 * c + v
-                nc.scalar.activation(h_turned[t][:, block(b)], dp_ps[t, c][:, block(v)], ACT.Copy, scale=uw_col[:, b, 1:2])
+                nc.scalar.activation(h_turned[t, c][:, block(v)], dp_ps[t, c][:, block(v)], ACT.Copy, scale=uw_col[:, b, 1:2])
 
         def h_back(t):
-            h[t] = turn(bank("h_ps%d" % t, "s%d" % t), [h_turned[t][:, block(b)] for b in range(PACK)])
+            h[t] = turn(bank("h_ps%d" % t, "s%d" % t), [h_turned[t, b // 2][:, block(b % 2)] for b in range(PACK)])
 
         def scaled(target, source, factor, t):
             nc.scalar.activation(column(target, t), column(source, t), ACT.Copy, scale=column(factor, t))
@@ -235,10 +236,11 @@ def tile_attend_gslot_q_kernel(tc, qT, kT, dp, us, ts, wt, offs, out):
             logits(t, heads[t], half(0))
         for t in range(2):
             logits(t, scores[t], half(1))
-        h_make(0, 1)
         for t in range(2):
             maximum(t)
-            exponentials(t)
+        exponentials(0)
+        h_make(0, 1, "z0")
+        exponentials(1)
         h_back(0)
         for c in range(2):
             h_make(1, c)

@@ -62,16 +62,18 @@ def tile_attend_gslot_q_kernel(tc, qT, kT, dp, us, ts, wt, offs, out):
             nc.sync.dma_start(k_plane[j][:], k_rows[:, j, :])
         q_raw = tiles("q_raw", 2, [P, PACK, HALF], F32)
         q_rows = qT.rearrange("(p j) r -> p j r", j=PACK)
-        dp_sb = {t: tile("dp_sb%d" % t, [P, R], F32) for t in range(1, PACK)}
         dp_rows = dp.rearrange("(s t) r -> s t r", t=PACK)
         for c in range(2):
             nc.sync.dma_start(q_raw[c][:], q_rows[:, :, half(c)])
+        dp_sb = {t: tile("dp_sb%d" % t, [P, R], F32) for t in range(1, LAST)}
         dp_first = tiles("dp_first", 2, [P, HALF], F32)
+        dp_last = tiles("dp_last", 2, [P, HALF], F32)
         nc.sync.dma_start(dp_first[0][:], dp_rows[:, 0, half(0)])
-        nc.sync.dma_start(dp_sb[LAST][:], dp_rows[:, LAST, :])
+        nc.sync.dma_start(dp_last[0][:], dp_rows[:, LAST, half(0)])
+        nc.sync.dma_start(dp_sb[2][:], dp_rows[:, 2, :])
         nc.sync.dma_start(dp_first[1][:], dp_rows[:, 0, half(1)])
-        for t in (2, 1):
-            nc.sync.dma_start(dp_sb[t][:], dp_rows[:, t, :])
+        nc.sync.dma_start(dp_sb[1][:], dp_rows[:, 1, :])
+        nc.sync.dma_start(dp_last[1][:], dp_rows[:, LAST, half(1)])
 
         ident = tile("ident", [P, P], F32)
         make_identity(nc, ident[:])
@@ -228,10 +230,11 @@ def tile_attend_gslot_q_kernel(tc, qT, kT, dp, us, ts, wt, offs, out):
         score(scores[LAST], LAST, slice(0, R))
         for c, on in enumerate(("h1", "h2")):
             dp_turn(1, c, dp_sb[1][:, half(c)], on)
-        h[LAST] = tile("h_last", [P, R], F32, "q_raw0")
-        nc.gpsimd.tensor_tensor(h[LAST][:], dp_sb[LAST][:], wt_sb[:], ALU.mult)
-        h[2] = tile("h_third", [P, R], F32, "dp_sb3")
+        h[LAST] = tile("h_last", [P, R], F32)
+        nc.vector.tensor_tensor(h[LAST][:, half(0)], dp_last[0][:], wt_sb[:, half(0)], ALU.mult)
+        h[2] = tile("h_third", [P, R], F32, "dp_last0")
         nc.gpsimd.tensor_tensor(h[2][:], dp_sb[2][:], wt_sb[:], ALU.mult)
+        nc.gpsimd.tensor_tensor(h[LAST][:, half(1)], dp_last[1][:], wt_sb[:, half(1)], ALU.mult)
         for t in range(2):
             logits(t, heads[t], half(0))
         for t in range(2):

@@ -18,6 +18,7 @@ P = 128
 PACK = 4
 D, R, SLOTS, TOKENS = 512, 512, 512, 2048
 HALF = R // 2
+QUAD = P // PACK
 LAST = PACK - 1
 FLOPS = 2 * 2 * D * R * SLOTS
 
@@ -48,15 +49,16 @@ def tile_attend_gslot_q_kernel(tc, qT, kT, dp, us, ts, wt, offs, out):
 
         offsets = sb.tile([P, SLOTS // 16], U16, name="offsets")
         ts_row = tile("ts_row", [P, TOKENS], F32)
-        uw_row = tile("uw_row", [P, R], F32)
-        nc.vector.memset(uw_row[0:P - 2, :], 0.0)
+        uw_rows = tile("uw_rows", [P, P], F32)
+        for b in range(PACK):
+            nc.vector.memset(uw_rows[b * QUAD:(b + 1) * QUAD - 2, :], 0.0)
         nc.vector.memset(ts_row[0:P - 1, :], 0.0)
         k_plane = tiles("k_plane", PACK, [P, TOKENS], F32)
         k_rows = kT.rearrange("(p j) n -> p j n", j=PACK)
         nc.sync.dma_start(k_plane[0][:], k_rows[:, 0, :])
         nc.sync.dma_start(offsets[:], offs)
-        nc.sync.dma_start(uw_row[P - 2:P - 1, :], us[0:1, :])
-        nc.sync.dma_start(uw_row[P - 1:P, :], wt[0:1, :])
+        for m, vector in enumerate((us, wt)):
+            nc.sync.dma_start(uw_rows[QUAD - 2 + m:P:QUAD, :], vector[0:1, :].rearrange("o (b x) -> (o b) x", b=PACK))
         nc.sync.dma_start(ts_row[P - 1:P, :], ts[0:1, :])
         for j in range(1, PACK):
             nc.sync.dma_start(k_plane[j][:], k_rows[:, j, :])
@@ -85,9 +87,10 @@ def tile_attend_gslot_q_kernel(tc, qT, kT, dp, us, ts, wt, offs, out):
                 nc.tensor.transpose(target[:, block(x)], blocks[x], ident[:])
             return target
 
-        uw_ps = turn(bank("uw_ps", "h0"), [uw_row[:, block(b)] for b in range(PACK)])
+        uw_ps = bank("uw_ps", "s0")
+        nc.tensor.transpose(uw_ps[:, 0:P], uw_rows[:], ident[:])
         uw_col = tile("uw_col", [P, PACK, 2], F32)
-        nc.scalar.activation(uw_col[:], uw_ps[:].rearrange("x (b m) -> x b m", b=PACK)[:, :, P - 2:P], ACT.Copy)
+        nc.scalar.activation(uw_col[:], uw_ps[:, 0:P].rearrange("x (b m) -> x b m", b=PACK)[:, :, QUAD - 2:QUAD], ACT.Copy)
 
         def spread(name, which, on):
             turned = turn(bank(name + "_ps", on), [uw_col[:, b, which:which + 1].to_broadcast([P, P]) for b in range(PACK)])
@@ -98,14 +101,18 @@ def tile_attend_gslot_q_kernel(tc, qT, kT, dp, us, ts, wt, offs, out):
         us_sb = spread("us_sb", 0, "h1")
         wt_sb = spread("wt_sb", 1, "h2")
 
-        ts_listed = tile("ts_listed", [P, SLOTS], F32, "uw_row")
+        ts_listed = tile("ts_listed", [P, SLOTS], F32, "uw_rows")
         nc.scalar.activation(ts_listed[:], ts_row[:].indirect(offsets[:]), ACT.Copy)
         ts_ps = turn(bank("ts_ps", "h0"), [ts_listed[:, t::PACK] for t in range(PACK)])
         ts_col = tile("ts_col", [P, PACK], F32)
         nc.scalar.copy(ts_col[:], ts_ps[:, P - 1::P])
-        ts_us = tiles("ts_us", PACK, [P, R], F32)
-        for t in range(PACK):
+        ts_us = dict(enumerate(tiles("ts_us", 2, [P, R], F32)))
+
+        def ts_us_make(t):
             nc.scalar.activation(ts_us[t][:], us_sb[:], ACT.Copy, scale=column(ts_col, t))
+
+        for t in range(2):
+            ts_us_make(t)
 
         k_words = tile("k_words", [P, PACK, P, PACK], BF16)
         kt_scales = tiles("kt_scales", PACK, [P, P], U8)
@@ -221,6 +228,10 @@ def tile_attend_gslot_q_kernel(tc, qT, kT, dp, us, ts, wt, offs, out):
         q_quantise(0)
         q_quantise(1)
         kt_quantise(LAST, "q_words0")
+        ts_us_late = tile("ts_us_late", [P, 2, R], F32, "q_words1")
+        for t in range(2, PACK):
+            ts_us[t] = ts_us_late[:, t - 2, :]
+            ts_us_make(t)
         for t in range(2):
             score(heads[t], t, half(0))
         for t in range(2):

@@ -20,6 +20,7 @@ D, R, SLOTS, TOKENS = 512, 512, 512, 2048
 HALF = R // 2
 QUAD = P // PACK
 LAST = PACK - 1
+SHARE = 64
 FLOPS = 2 * 2 * D * R * SLOTS
 
 
@@ -64,18 +65,16 @@ def tile_attend_gslot_q_kernel(tc, qT, kT, dp, us, ts, wt, offs, out):
             nc.sync.dma_start(k_plane[j][:], k_rows[:, j, :])
         q_raw = tiles("q_raw", 2, [P, PACK, HALF], F32)
         q_rows = qT.rearrange("(p j) r -> p j r", j=PACK)
+        dp_sb = {t: tile("dp_sb%d" % t, [P, R], F32) for t in range(1, PACK)}
         dp_rows = dp.rearrange("(s t) r -> s t r", t=PACK)
         for c in range(2):
             nc.sync.dma_start(q_raw[c][:], q_rows[:, :, half(c)])
-        dp_sb = {t: tile("dp_sb%d" % t, [P, R], F32) for t in range(1, LAST)}
         dp_first = tiles("dp_first", 2, [P, HALF], F32)
-        dp_last = tiles("dp_last", 2, [P, HALF], F32)
         nc.sync.dma_start(dp_first[0][:], dp_rows[:, 0, half(0)])
-        nc.sync.dma_start(dp_last[0][:], dp_rows[:, LAST, half(0)])
-        nc.sync.dma_start(dp_sb[2][:], dp_rows[:, 2, :])
+        nc.sync.dma_start(dp_sb[LAST][:], dp_rows[:, LAST, :])
         nc.sync.dma_start(dp_first[1][:], dp_rows[:, 0, half(1)])
-        nc.sync.dma_start(dp_sb[1][:], dp_rows[:, 1, :])
-        nc.sync.dma_start(dp_last[1][:], dp_rows[:, LAST, half(1)])
+        for t in (2, 1):
+            nc.sync.dma_start(dp_sb[t][:], dp_rows[:, t, :])
 
         ident = tile("ident", [P, P], F32)
         make_identity(nc, ident[:])
@@ -92,14 +91,14 @@ def tile_attend_gslot_q_kernel(tc, qT, kT, dp, us, ts, wt, offs, out):
         uw_col = tile("uw_col", [P, PACK, 2], F32)
         nc.scalar.activation(uw_col[:], uw_ps[:, 0:P].rearrange("x (b m) -> x b m", b=PACK)[:, :, QUAD - 2:QUAD], ACT.Copy)
 
-        def spread(name, which, on):
+        def spread(name, which, on, copy):
             turned = turn(bank(name + "_ps", on), [uw_col[:, b, which:which + 1].to_broadcast([P, P]) for b in range(PACK)])
             whole = tile(name, [P, R], F32)
-            nc.scalar.copy(whole[:], turned[:])
+            copy(whole[:], turned[:])
             return whole
 
-        us_sb = spread("us_sb", 0, "h1")
-        wt_sb = spread("wt_sb", 1, "h2")
+        us_sb = spread("us_sb", 0, "h1", nc.scalar.copy)
+        wt_sb = spread("wt_sb", 1, "h2", nc.vector.tensor_copy)
 
         ts_listed = tile("ts_listed", [P, SLOTS], F32, "uw_rows")
         nc.scalar.activation(ts_listed[:], ts_row[:].indirect(offsets[:]), ACT.Copy)
@@ -110,6 +109,7 @@ def tile_attend_gslot_q_kernel(tc, qT, kT, dp, us, ts, wt, offs, out):
 
         def ts_us_make(t):
             nc.scalar.activation(ts_us[t][:], us_sb[:], ACT.Copy, scale=column(ts_col, t))
+
 
         for t in range(2):
             ts_us_make(t)
@@ -151,11 +151,16 @@ def tile_attend_gslot_q_kernel(tc, qT, kT, dp, us, ts, wt, offs, out):
         q_words = tiles("q_words", 2, [P, HALF, PACK], BF16)
         q_codes = tile("q_codes", [P, R], U32)
         q_scales = tile("q_scales", [P, R], U8)
-        for c, copy in enumerate((nc.scalar.copy, nc.vector.tensor_copy)):
+
+        def q_lay(c, first, end, copy):
             copy(
-                q_words[c][:].rearrange("p (n x) j -> p n j x", x=2),
-                q_raw[c][:].rearrange("p j (n x) -> p n j x", x=2),
+                q_words[c][:, first:end, :].rearrange("p (n x) j -> p n j x", x=2),
+                q_raw[c][:, :, first:end].rearrange("p j (n x) -> p n j x", x=2),
             )
+
+        q_lay(0, 0, HALF, nc.scalar.copy)
+        q_lay(1, 0, HALF - SHARE, nc.vector.tensor_copy)
+        q_lay(1, HALF - SHARE, HALF, nc.scalar.copy)
         kt_lay(LAST, kt_last_ps, "q_raw0")
 
         def q_quantise(c):
@@ -241,11 +246,10 @@ def tile_attend_gslot_q_kernel(tc, qT, kT, dp, us, ts, wt, offs, out):
         score(scores[LAST], LAST, slice(0, R))
         for c, on in enumerate(("h1", "h2")):
             dp_turn(1, c, dp_sb[1][:, half(c)], on)
-        h[LAST] = tile("h_last", [P, R], F32)
-        nc.vector.tensor_tensor(h[LAST][:, half(0)], dp_last[0][:], wt_sb[:, half(0)], ALU.mult)
-        h[2] = tile("h_third", [P, R], F32, "dp_last0")
+        h[LAST] = tile("h_last", [P, R], F32, "q_raw0")
+        nc.gpsimd.tensor_tensor(h[LAST][:], dp_sb[LAST][:], wt_sb[:], ALU.mult)
+        h[2] = tile("h_third", [P, R], F32, "dp_sb3")
         nc.gpsimd.tensor_tensor(h[2][:], dp_sb[2][:], wt_sb[:], ALU.mult)
-        nc.gpsimd.tensor_tensor(h[LAST][:, half(1)], dp_last[1][:], wt_sb[:, half(1)], ALU.mult)
         for t in range(2):
             logits(t, heads[t], half(0))
         for t in range(2):

from contextlib import ExitStack

import concourse.mybir as mybir
from concourse.masks import make_identity

F32 = mybir.dt.float32
BF16 = mybir.dt.bfloat16
U32 = mybir.dt.uint32
U16 = mybir.dt.uint16
U8 = mybir.dt.uint8
E4M3 = mybir.dt.float8_e4m3fn_x4
E5M2 = mybir.dt.float8_e5m2_x4
ALU = mybir.AluOpType
ACT = mybir.ActivationFunctionType
AX = mybir.AxisListType

P = 128
PACK = 4
D, R, SLOTS, TOKENS = 512, 512, 512, 2048
HALF = R // 2
QUAD = P // PACK
LAST = PACK - 1
SHARE = 64
FLOPS = 2 * 2 * D * R * SLOTS


def tile_attend_gslot_q_kernel(tc, qT, kT, dp, us, ts, wt, offs, out):
    nc = tc.nc
    with ExitStack() as ctx:
        sb = ctx.enter_context(tc.tile_pool(name="sb", bufs=1))
        ps = ctx.enter_context(tc.psum_pool(name="ps", bufs=1))

        def tile(name, shape, dtype, on=None):
            return sb.tile(shape, dtype, name=name, tag=on or name, align_bytes=64)

        def tiles(name, count, shape, dtype):
            return [tile("%s%d" % (name, x), shape, dtype) for x in range(count)]

        def bank(name, on):
            return ps.tile([P, R], F32, name=name, tag=on)

        def block(x):
            return slice(x * P, (x + 1) * P)

        def half(c):
            return slice(c * HALF, (c + 1) * HALF)

        def column(stats, x):
            return stats[:, x:x + 1]

        offsets = sb.tile([P, SLOTS // 16], U16, name="offsets")
        ts_row = tile("ts_row", [P, TOKENS], F32)
        uw_rows = tile("uw_rows", [P, P], F32)
        for b in range(PACK):
            nc.vector.memset(uw_rows[b * QUAD:(b + 1) * QUAD - 2, :], 0.0)
        nc.vector.memset(ts_row[0:P - 1, :], 0.0)
        k_plane = tiles("k_plane", PACK, [P, TOKENS], F32)
        k_rows = kT.rearrange("(p j) n -> p j n", j=PACK)
        nc.sync.dma_start(k_plane[0][:], k_rows[:, 0, :])
        nc.sync.dma_start(offsets[:], offs)
        for m, vector in enumerate((us, wt)):
            nc.sync.dma_start(uw_rows[QUAD - 2 + m:P:QUAD, :], vector[0:1, :].rearrange("o (b x) -> (o b) x", b=PACK))
        nc.sync.dma_start(ts_row[P - 1:P, :], ts[0:1, :])
        for j in range(1, PACK):
            nc.sync.dma_start(k_plane[j][:], k_rows[:, j, :])
        q_raw = tiles("q_raw", 2, [P, PACK, HALF], F32)
        q_rows = qT.rearrange("(p j) r -> p j r", j=PACK)
        dp_sb = {t: tile("dp_sb%d" % t, [P, R], F32) for t in range(1, PACK)}
        dp_rows = dp.rearrange("(s t) r -> s t r", t=PACK)
        for c in range(2):
            nc.sync.dma_start(q_raw[c][:], q_rows[:, :, half(c)])
        dp_first = tiles("dp_first", 2, [P, HALF], F32)
        nc.sync.dma_start(dp_first[0][:], dp_rows[:, 0, half(0)])
        nc.sync.dma_start(dp_sb[LAST][:], dp_rows[:, LAST, :])
        nc.sync.dma_start(dp_first[1][:], dp_rows[:, 0, half(1)])
        for t in (2, 1):
            nc.sync.dma_start(dp_sb[t][:], dp_rows[:, t, :])

        ident = tile("ident", [P, P], F32)
        make_identity(nc, ident[:])
        ident16 = tile("ident16", [P, P], BF16)
        make_identity(nc, ident16[:])

        def turn(target, blocks):
            for x in range(PACK):
                nc.tensor.transpose(target[:, block(x)], blocks[x], ident[:])
            return target

        uw_ps = bank("uw_ps", "s0")
        nc.tensor.transpose(uw_ps[:, 0:P], uw_rows[:], ident[:])
        uw_col = tile("uw_col", [P, PACK, 2], F32)
        nc.scalar.activation(uw_col[:], uw_ps[:, 0:P].rearrange("x (b m) -> x b m", b=PACK)[:, :, QUAD - 2:QUAD], ACT.Copy)

        def spread(name, which, on, copy):
            turned = turn(bank(name + "_ps", on), [uw_col[:, b, which:which + 1].to_broadcast([P, P]) for b in range(PACK)])
            whole = tile(name, [P, R], F32)
            copy(whole[:], turned[:])
            return whole

        us_sb = spread("us_sb", 0, "h1", nc.scalar.copy)
        wt_sb = spread("wt_sb", 1, "h2", nc.vector.tensor_copy)

        ts_listed = tile("ts_listed", [P, SLOTS], F32, "uw_rows")
        nc.scalar.activation(ts_listed[:], ts_row[:].indirect(offsets[:]), ACT.Copy)
        ts_ps = turn(bank("ts_ps", "h0"), [ts_listed[:, t::PACK] for t in range(PACK)])
        ts_col = tile("ts_col", [P, PACK], F32)
        nc.scalar.copy(ts_col[:], ts_ps[:, P - 1::P])
        ts_us = dict(enumerate(tiles("ts_us", 2, [P, R], F32)))

        def ts_us_make(t):
            nc.scalar.activation(ts_us[t][:], us_sb[:], ACT.Copy, scale=column(ts_col, t))


        for t in range(2):
            ts_us_make(t)

        k_words = tile("k_words", [P, PACK, P, PACK], BF16)
        kt_scales = tiles("kt_scales", PACK, [P, P], U8)
        kt_words, kt_codes = {}, {}

        def k_gather(j):
            nc.vector.tensor_copy(
                k_words[:, :, :, j].rearrange("p t s -> p s t"), k_plane[j][:].indirect(offsets[:])
            )

        def kt_turn(j, on):
            turned = ps.tile([P, 2 * R], BF16, name="kt_plane%d" % j, tag=on)
            for t in range(PACK):
                nc.tensor.transpose(turned[:, block(t)], k_words[:, t, :, j], ident16[:])
            return turned[:, 0:R].rearrange("s (t p) -> s p t", t=PACK)

        def kt_lay(j, turned, on=None):
            kt_words[j] = tile("kt_words%d" % j, [P, P, PACK], BF16, on)
            nc.scalar.copy(kt_words[j][:], turned)

        def kt_quantise(j, on):
            kt_codes[j] = tile("kt_codes%d" % j, [P, P], U32, on)
            nc.vector.quantize_mx(kt_codes[j][:].bitcast(E4M3), kt_scales[j][:], kt_words[j][:].rearrange("s p t -> s (p t)"))

        for j in range(PACK):
            k_gather(j)
            if j > 0:
                kt_quantise(j - 1, "k_plane%d" % j)
            if j < LAST:
                kt_lay(j, kt_turn(j, "s%d" % j))
        kt_last_ps = kt_turn(LAST, "x")
        k_codes = tile("k_codes", [P, SLOTS], U32)
        k_scales = tile("k_scales", [P, SLOTS], U8)
        nc.vector.quantize_mx(k_codes[:].bitcast(E4M3), k_scales[:], k_words[:].rearrange("p t s j -> p (t s j)"))

        q_words = tiles("q_words", 2, [P, HALF, PACK], BF16)
        q_codes = tile("q_codes", [P, R], U32)
        q_scales = tile("q_scales", [P, R], U8)

        def q_lay(c, first, end, copy):
            copy(
                q_words[c][:, first:end, :].rearrange("p (n x) j -> p n j x", x=2),
                q_raw[c][:, :, first:end].rearrange("p j (n x) -> p n j x", x=2),
            )

        q_lay(0, 0, HALF, nc.scalar.copy)
        q_lay(1, 0, HALF - SHARE, nc.vector.tensor_copy)
        q_lay(1, HALF - SHARE, HALF, nc.scalar.copy)
        kt_lay(LAST, kt_last_ps, "q_raw0")

        def q_quantise(c):
            nc.vector.quantize_mx(q_codes[:, half(c)].bitcast(E4M3), q_scales[:, half(c)], q_words[c][:].rearrange("p r j -> p (r j)"))

        def score(target, t, cols):
            nc.tensor.matmul_mx(
                target[:, cols], lhsT=k_codes[:, block(t)].bitcast(E4M3), lhsT_scale=k_scales[:, block(t)],
                rhs=q_codes[:, cols].bitcast(E4M3), rhs_scale=q_scales[:, cols], start=True, stop=True,
            )

        z = tiles("z", PACK, [P, R], F32)
        e = tiles("e", PACK, [P, R], F32)
        neg_max = tiles("neg_max", PACK, [P, 1], F32)
        tot = tile("tot", [P, PACK], F32)
        rtot = tile("rtot", [P, PACK], F32)
        rtot2 = tile("rtot2", [P, LAST], F32)
        neg_sum = tile("neg_sum", [P, LAST], F32)
        bias = tile("bias", [P, LAST], F32)
        left = tiles("left", 2, [P, PACK, HALF], F32)
        right = tile("right", [P, PACK, R], F32)
        h_turned = {}
        neg_eh = {}
        h, dp_ps = {}, {}

        def logits(t, source, cols):
            nc.vector.tensor_tensor(z[t][:, cols], source[:, cols], ts_us[t][:, cols], ALU.mult)

        def maximum(t):
            nc.vector.tensor_reduce(neg_max[t][:], z[t][:], AX.X, ALU.max, negate=True)

        def exponentials(t):
            nc.scalar.activation(e[t][:], z[t][:], ACT.Exp, bias=neg_max[t][:], accum_out=column(tot, t))

        def reciprocals(first, end):
            nc.vector.reciprocal(rtot[:, first:end], tot[:, first:end])

        def dp_turn(t, c, source, on):
            dp_ps[t, c] = bank("dp_ps%d_%d" % (t, c), on)
            for v in range(2):
                nc.tensor.transpose(dp_ps[t, c][:, block(v)], source[:, block(v)], ident[:])

        def h_make(t, c, on=None):
            h_turned[t, c] = tile("h_turned%d_%d" % (t, c), [P, HALF], F32, on)
            for v in range(2):
                b = 2 * c + v
                nc.scalar.activation(h_turned[t, c][:, block(v)], dp_ps[t, c][:, block(v)], ACT.Copy, scale=uw_col[:, b, 1:2])

        def h_back(t):
            h[t] = turn(bank("h_ps%d" % t, "s%d" % t), [h_turned[t, b // 2][:, block(b % 2)] for b in range(PACK)])

        def scaled(target, source, factor, t):
            nc.scalar.activation(column(target, t), column(source, t), ACT.Copy, scale=column(factor, t))

        def row_sum(t, on=None):
            neg_eh[t] = tile("neg_eh%d" % t, [P, R], F32, on)
            nc.vector.scalar_tensor_tensor(
                neg_eh[t][:], e[t][:], -1.0, h[t][:], ALU.mult, ALU.mult, accum_out=column(neg_sum, t)
            )

        def left_on_scalar(t, c):
            nc.scalar.activation(
                left[c][:, t, :], h[t][:, half(c)], ACT.Identity, bias=column(bias, t), scale=column(rtot, t)
            )

        dp_turn(0, 0, dp_first[0], "s1")
        h_make(0, 0)
        heads = [bank("head%d" % t, on) for t, on in enumerate(("h0", "s0"))]
        scores = [bank("scores%d" % t, on) for t, on in enumerate(("h1", "h2", "s2", "s3"))]
        q_quantise(0)
        q_quantise(1)
        kt_quantise(LAST, "q_words0")
        ts_us_late = tile("ts_us_late", [P, 2, R], F32, "q_words1")
        for t in range(2, PACK):
            ts_us[t] = ts_us_late[:, t - 2, :]
            ts_us_make(t)
        for t in range(2):
            score(heads[t], t, half(0))
        for t in range(2):
            score(scores[t], t, half(1))
        dp_turn(0, 1, dp_first[1], "h0")
        score(scores[2], 2, slice(0, R))
        score(scores[LAST], LAST, slice(0, R))
        for c, on in enumerate(("h1", "h2")):
            dp_turn(1, c, dp_sb[1][:, half(c)], on)
        h[LAST] = tile("h_last", [P, R], F32, "q_raw0")
        nc.gpsimd.tensor_tensor(h[LAST][:], dp_sb[LAST][:], wt_sb[:], ALU.mult)
        h[2] = tile("h_third", [P, R], F32, "dp_sb3")
        nc.gpsimd.tensor_tensor(h[2][:], dp_sb[2][:], wt_sb[:], ALU.mult)
        for t in range(2):
            logits(t, heads[t], half(0))
        for t in range(2):
            logits(t, scores[t], half(1))
        for t in range(2):
            maximum(t)
        exponentials(0)
        h_make(0, 1, "z0")
        exponentials(1)
        h_back(0)
        for c in range(2):
            h_make(1, c)
        h_back(1)
        for t in range(2, PACK):
            logits(t, scores[t], slice(0, R))
        for t in range(2, PACK):
            maximum(t)
            exponentials(t)
        for t in range(2):
            nc.gpsimd.tensor_tensor(right[:, t, :], e[t][:], ts_us[t][:], ALU.mult)

        reciprocals(0, 2)
        for t in range(2):
            scaled(rtot2, rtot, rtot, t)
        row_sum(0)
        scaled(bias, neg_sum, rtot2, 0)
        left_on_scalar(0, 0)
        row_sum(1)
        scaled(bias, neg_sum, rtot2, 1)
        left_on_scalar(1, 0)
        reciprocals(2, LAST)
        reciprocals(LAST, PACK)
        row_sum(2, "ts_us1")
        nc.scalar.activation(right[:, LAST, half(0)], ts_us[LAST][:, half(0)], ACT.Copy, scale=column(rtot, LAST))
        neg_mean = tile("neg_mean", [P, PACK], F32)
        scaled(neg_mean, neg_sum, rtot, 2)
        nc.scalar.activation(left[0][:, 2, :], h[2][:, half(0)], ACT.Identity, bias=column(neg_mean, 2))

        ph = tile("ph", [P, R], F32)
        mean = tile("mean", [P, 1], F32)

        def right_third(c):
            nc.vector.scalar_tensor_tensor(
                right[:, 2, half(c)], e[2][:, half(c)], column(rtot, 2), ts_us[2][:, half(c)], ALU.mult, ALU.mult
            )

        right_third(0)
        nc.vector.scalar_tensor_tensor(
            ph[:], e[LAST][:], column(rtot, LAST), h[LAST][:], ALU.mult, ALU.mult, accum_out=mean[:]
        )
        right_third(1)
        for c in range(2):
            nc.vector.scalar_tensor_tensor(
                left[c][:, LAST, :], h[LAST][:, half(c)], mean[:], e[LAST][:, half(c)], ALU.subtract, ALU.mult
            )
        for t in range(2):
            left_on_scalar(t, 1)
        nc.scalar.activation(left[1][:, 2, :], h[2][:, half(1)], ACT.Identity, bias=column(neg_mean, 2))
        nc.scalar.activation(right[:, LAST, half(1)], ts_us[LAST][:, half(1)], ACT.Copy, scale=column(rtot, LAST))

        out_rows = out.rearrange("(p j) r -> p j r", j=PACK)
        g_words, g_codes, g_scales = {}, {}, {}

        def g_form(x, start=0, stop=P):
            first, end = x * P + start, x * P + stop
            if start == 0:
                g_words[x] = tile("g_words%d" % x, [P, P, PACK], BF16, "g_words%d" % (x % 2))
            nc.vector.tensor_tensor(
                g_words[x][:, start:stop, :].rearrange("s (n x) t -> s n t x", x=2),
                left[first // HALF][:, :, first % HALF:first % HALF + end - first].rearrange("s t (n x) -> s n t x", x=2),
                right[:, :, first:end].rearrange("s t (n x) -> s n t x", x=2),
                ALU.mult,
            )

        def g_quantise(x, start=0, stop=P):
            if start == 0:
                g_codes[x] = tile("g_codes%d" % x, [P, P], U32)
                g_scales[x] = tile("g_scales%d" % x, [P, P], U8)
            nc.vector.quantize_mx(
                g_codes[x][:, start:stop].bitcast(E5M2), g_scales[x][:, start:stop],
                g_words[x][:, start:stop, :].rearrange("s r t -> s (r t)"),
            )

        def passes(x, first, end, on):
            acc = bank("acc%d_%d" % (x, first), on)
            for j in range(first, end):
                nc.tensor.matmul_mx(
                    acc[:, block(j - first)], lhsT=kt_codes[j][:].bitcast(E4M3), lhsT_scale=kt_scales[j][:],
                    rhs=g_codes[x][:].bitcast(E5M2), rhs_scale=g_scales[x][:], start=True, stop=True,
                )
            return acc[:, 0:(end - first) * P]

        def product(x, first, end, on, copy):
            acc = passes(x, first, end, on)
            result = tile("result%d_%d" % (x, first), [P, end - first, P], F32)
            copy(result[:].rearrange("p j r -> p (j r)"), acc)
            nc.sync.dma_start(out_rows[:, first:end, block(x)], result[:])

        g_form(0)
        for x in range(LAST):
            g_form(x + 1, 0, P // 2)
            g_quantise(x)
            product(x, 0, 2, ("x", "h1", "s2")[x], nc.scalar.copy)
            product(x, 2, PACK, ("h0", "h2", "s3")[x], nc.scalar.copy)
            g_form(x + 1, P // 2, P)
        g_quantise(LAST, 0, P // 2)
        g_quantise(LAST, P // 2, P)
        product(LAST, 0, 2, "x", nc.scalar.copy)
        result_last = tile("result_last", [P, 2, P], F32)
        for v in range(2):
            nc.vector.tensor_copy(result_last[:, v, :], passes(LAST, 2 + v, 3 + v, ("s0", "s1")[v]))
        nc.sync.dma_start(out_rows[:, 2:PACK, block(LAST)], result_last[:])
